import numpy as np
import ml_dtypes


def mxq(x, axis, fmt="e4m3"):
    dtype, down = {"e4m3": (ml_dtypes.float8_e4m3fn, 7), "e5m2": (ml_dtypes.float8_e5m2, 14)}[fmt]
    v = np.moveaxis(np.asarray(x, np.float32).astype(ml_dtypes.bfloat16).astype(np.float64), axis, -1)
    blocks = v.reshape(v.shape[:-1] + (-1, 32))
    amax = np.abs(blocks).max(-1, keepdims=True)
    byte = np.maximum(np.where(amax > 0, np.frexp(amax)[1] - 1 + 127, 0) - down, 1)
    scale = np.exp2(byte - 127.0)
    codes = (blocks / scale).astype(np.float32).astype(dtype).astype(np.float64)
    return np.moveaxis((codes * scale).reshape(v.shape), -1, axis)


WIDE = False


def mx_kscale(k):
    if not WIDE:
        return np.ones(k)
    levels = np.array([10, -10, 5, -5, 0])
    if k % 512:
        return np.exp2(np.random.permutation(np.resize(levels, k // 32))).repeat(32)
    a = np.empty((k // 512, 16))
    for p in range(k // 512):
        a[p, :8] = np.random.permutation(np.resize(levels, 8))
        for g in range(8):
            far = levels[np.abs(levels - a[p, g]) >= 10]
            a[p, g + 8] = far[np.random.randint(len(far))]
    return np.exp2(a.ravel()).repeat(32)


def f64(x):
    return np.asarray(x).astype(np.float64)


def striped(idx):
    return np.tile(idx.reshape(-1, 16).T, (8, 1)).astype(np.uint16)


def unstriped(offs):
    return offs[:16].T.reshape(-1).astype(np.int64)


E2M1 = np.array([0.0, 0.5, 1.0, 1.5, 2.0, 3.0, 4.0, 6.0, -0.0, -0.5, -1.0, -1.5, -2.0, -3.0, -4.0, -6.0])


def pack_weight(w, fmt):
    k, n = w.shape
    w = f64(np.asarray(w, np.float32).astype(ml_dtypes.bfloat16)).reshape(k // 32, 32, n)
    amax = np.abs(w).max(1)
    if fmt == "e4m3":
        byte = np.frexp(amax)[1] - 1 + 127 - 7
    else:
        mant, ex = np.frexp(amax / 6.0)
        byte = np.where(mant > 0.5, ex, ex - 1) + 127
    byte = np.clip(np.where(amax > 0, byte, 1), 1, 254)
    scaled = (w * np.exp2(127.0 - byte)[:, None, :]).reshape(k, n).astype(np.float32)
    by_word = np.ascontiguousarray(scaled.reshape(k // 512, 128, 4, n).transpose(0, 1, 3, 2))
    if fmt == "e4m3":
        words = by_word.astype(ml_dtypes.float8_e4m3fn).view(np.uint8)
    else:
        c = by_word.astype(ml_dtypes.float4_e2m1fn).view(np.uint8) & 0xF
        words = (c[..., 0::2] | (c[..., 1::2] << 4)).reshape(k // 512, 128, 2 * n)
    return np.ascontiguousarray(words), np.ascontiguousarray(byte.astype(np.uint8).reshape(k // 512, 16, n))


def unpack_weight(words, scales, fmt):
    g, _, n = scales.shape
    words = np.ascontiguousarray(words).reshape(g, 128, n, -1)
    if fmt == "e4m3":
        vals = words.view(ml_dtypes.float8_e4m3fn).astype(np.float64)
    else:
        nib = np.empty((g, 128, n, 4), np.uint8)
        nib[..., 0::2] = words & 0xF
        nib[..., 1::2] = words >> 4
        vals = E2M1[nib]
    vals = vals * np.repeat(np.exp2(scales.astype(np.float64) - 127.0), 8, axis=1)[..., None]
    return vals.transpose(0, 1, 3, 2).reshape(g * 512, n)


def gelu(v):
    return 0.5 * v * (1.0 + np.tanh(np.sqrt(2.0 / np.pi) * (v + 0.044715 * v**3)))


K, M, T, S = 1536, 512, 4096, 2048


def setup_inputs():
    n = np.random.standard_normal
    s = mx_kscale(K)[:, None]
    w = n((K, M)) / np.sqrt(K) / s
    v = pack_weight(n((K, T)) * s, "e4m3")
    p_w4 = pack_weight(w[512:], "e2m1")
    return {
        "tab_words": v[0],
        "tab_scales": v[1],
        "w8": (w[:512]).astype(np.float32),
        "w4_words": p_w4[0],
        "w4_scales": p_w4[1],
        "ts": np.tile(np.exp(0.5 * n(T)), (128, 1)).astype(np.float32),
        "b": (0.3 * n(512)).astype(np.float32),
        "offs": striped(np.random.permutation(T)[:S]),
    }


def reference(tab_words, tab_scales, w8, w4_words, w4_scales, ts, b, offs):
    tab_ = unpack_weight(tab_words, tab_scales, "e4m3")[:, unstriped(offs)]
    w8_ = mxq(f64(w8), 0, "e4m3")
    w4_ = unpack_weight(w4_words, w4_scales, "e2m1")
    y = w8_.T @ tab_[:512] + w4_.T @ tab_[512:]
    y = y * f64(ts)[0][unstriped(offs)]
    return gelu(y + f64(b)[:, None])

@@ -1,0 +1,208 @@
+from contextlib import ExitStack
+
+import concourse.mybir as mybir
+from concourse.masks import make_identity
+
+K, M, T, S = 1536, 512, 4096, 2048
+FLOPS = 2 * K * M * S
+
+F32 = mybir.dt.float32
+BF16 = mybir.dt.bfloat16
+I32 = mybir.dt.int32
+U32 = mybir.dt.uint32
+U16 = mybir.dt.uint16
+U8 = mybir.dt.uint8
+FP8X4 = mybir.dt.float8_e4m3fn_x4
+FP4X4 = mybir.dt.float4_e2m1fn_x4
+GELU = mybir.ActivationFunctionType.Gelu_apprx_tanh
+COPY = mybir.ActivationFunctionType.Copy
+MULT = mybir.AluOpType.mult
+
+P = 128
+NB = 512
+PASS_ORDER = (1, 2, 0)
+
+
+def tile_list_tabts_gelu_kernel(tc, tab_words, tab_scales, w8, w4_words, w4_scales, ts, b, offs, out):
+    nc = tc.nc
+    with ExitStack() as ctx:
+        keep = ctx.enter_context(tc.tile_pool(name="keep", bufs=1))
+        stage = ctx.enter_context(tc.tile_pool(name="stage", bufs=8))
+        psum = ctx.enter_context(tc.psum_pool(name="psum", bufs=1))
+
+        def bank(i):
+            return psum.tile([P, NB], F32, name="bank%d" % i, tag="bank%d" % i)
+
+        offsets = keep.tile([P, S // 16], U16, name="offsets")
+        nc.sync.dma_start(offsets[:], offs)
+
+        scale_rows = tab_scales.rearrange("a q t -> (a q) t").bitcast(I32)
+        scale_win = keep.tile([P, T // 4], I32, name="scale_win", align_bytes=64)
+        nc.sync.dma_start(scale_win[0:32, :], scale_rows[0:32, :])
+        nc.sync.dma_start(scale_win[64:96, :], scale_rows[16:48, :])
+        ts_rows = keep.tile([P, P], F32, name="ts_rows")
+        nc.sync.dma_start(ts_rows[:], ts[0:4, :].rearrange("a (c p) -> (a c) p", p=P))
+
+        table = {}
+        w8_raw = keep.tile([P, 4, M], F32, name="w8_raw")
+        for a in PASS_ORDER:
+            if a == 0:
+                nc.sync.dma_start(w8_raw[:], w8.rearrange("(p j) n -> p j n", j=4))
+            table[a] = keep.tile([P, T], I32, name="table%d" % a, align_bytes=64)
+            nc.sync.dma_start(table[a][:], tab_words[a].rearrange("p t i -> p (t i)").bitcast(I32))
+
+        warm = keep.tile([P, 2], F32, name="warm")
+        nc.vector.memset(warm[:, 0:1], 0.0)
+        nc.scalar.activation(warm[:, 1:2], warm[:, 0:1], GELU)
+        nc.vector.memset(scale_win[32:64, :], 0)
+        nc.vector.memset(scale_win[96:128, :], 0)
+        w4_plane = keep.tile([P, 2, M // 4], I32, name="w4_plane", align_bytes=64)
+        nc.vector.memset(w4_plane[:], 0)
+        planes = keep.tile([P, 3, S // 4], I32, name="planes", align_bytes=64)
+        nc.vector.memset(planes[:], 0)
+
+        ident = keep.tile([P, P], F32, name="ident")
+        make_identity(nc, ident[:])
+
+        w4 = keep.tile([P, 2, 2 * M], U8, name="w4", align_bytes=64)
+        nc.gpsimd.dma_start(w4[:].bitcast(I32), w4_words.rearrange("a p n -> p a n").bitcast(I32))
+        for q in range(4):
+            nc.gpsimd.dma_start(
+                w4_plane[32 * q : 32 * q + 4, :, :],
+                w4_scales[:, 4 * q : 4 * q + 4, :].rearrange("a r n -> r a n").bitcast(I32),
+            )
+        bias = keep.tile([P, 4], F32, name="bias")
+        with nc.allow_non_contiguous_dma(reason="one bias value a partition"):
+            nc.gpsimd.dma_start(bias[:], b.rearrange("(m p) -> p m", p=P))
+
+        ts_cols = keep.tile([P, 32], F32, name="ts_cols")
+        first = bank(0)
+        nc.tensor.transpose(first[:, 0:P], ts_rows[:], ident[:])
+        nc.scalar.copy(ts_cols[:], first[:, 0:32])
+        ts_win = keep.tile([P, T], F32, name="ts_win", align_bytes=64)
+        for g in range(T // NB):
+            spread = bank(1 + g % 4)
+            for c in range(4):
+                col = 4 * g + c
+                nc.tensor.transpose(spread[:, c * P : (c + 1) * P], ts_cols[:, col : col + 1].to_broadcast([P, P]), ident[:])
+            nc.scalar.copy(ts_win[:, g * NB : (g + 1) * NB], spread[:])
+
+        picked_scales = keep.tile([P, S // 4], I32, name="picked_scales", align_bytes=64)
+        nc.vector.tensor_copy(picked_scales[:].bitcast(U8), scale_win[:].bitcast(U8).indirect(offsets[:]))
+        for step, a in enumerate(PASS_ORDER):
+            for q in range(4):
+                row = 16 * a + 4 * q if a < 2 else 64 + 16 + 4 * q
+                eng = nc.scalar if 4 * step + q < 6 else nc.gpsimd
+                eng.dma_start(planes[32 * q : 32 * q + 4, a, :], picked_scales[row : row + 4, :])
+
+        picked = {}
+        picked_ts = {}
+        w8_codes = keep.tile([P, M], U32, name="w8_codes", align_bytes=64)
+        w8_plane = keep.tile([P, M], U8, name="w8_plane", align_bytes=64)
+
+        def cut(s):
+            return offsets[:, s * 32 : (s + 1) * 32]
+
+        def gather_words(a, s, slot=None):
+            name = "picked%d_%d" % (a, s)
+            picked[a, s] = keep.tile([P, NB], U32, name=name, tag=slot or name, align_bytes=64)
+            nc.vector.tensor_copy(picked[a, s][:], table[a][:].bitcast(U32).indirect(cut(s)))
+
+        def gather_ts(s, slot=None):
+            name = "picked_ts%d" % s
+            picked_ts[s] = keep.tile([P, NB], F32, name=name, tag=slot or name, align_bytes=64)
+            nc.vector.tensor_copy(picked_ts[s][:], ts_win[:].indirect(cut(s)))
+
+        def weights(a, n0, n1):
+            if a == 0:
+                return w8_codes[:, n0:n1].bitcast(FP8X4), w8_plane[:, n0:n1]
+            return w4[:, a - 1, 2 * n0 : 2 * n1].bitcast(FP4X4), w4_plane[:, a - 1, :].bitcast(U8)[:, n0:n1]
+
+        def tokens(a, j0, j1):
+            return picked[a, j0 // NB][:, j0 % NB : j0 % NB + j1 - j0].bitcast(FP8X4), planes[:, a, :].bitcast(U8)[:, j0:j1]
+
+        def mm(acc, a, lhs, rhs):
+            nc.tensor.matmul_mx(
+                out=acc[:], lhsT=lhs[0], lhsT_scale=lhs[1], rhs=rhs[0], rhs_scale=rhs[1],
+                start=(a == PASS_ORDER[0]), stop=(a == PASS_ORDER[-1]),
+            )
+
+        def mm_turned(accs, a, s):
+            for i in range(4):
+                j0 = s * NB + i * P
+                mm(accs[i], a, tokens(a, j0, j0 + P), weights(a, 0, M))
+
+        def mm_direct(acc, a, s, m):
+            mm(acc, a, weights(a, m * P, (m + 1) * P), tokens(a, s * NB, (s + 1) * NB))
+
+        def finish(src, s, m):
+            res = stage.tile([P, NB], F32, name="res")
+            nc.scalar.activation(res[:], src, GELU, bias=bias[:, m : m + 1])
+            nc.sync.dma_start(out[m * P : (m + 1) * P, s * NB : (s + 1) * NB], res[:])
+
+        def scale_direct(acc, s, m):
+            y = stage.tile([P, NB], F32, name="y")
+            nc.vector.tensor_tensor(y[:], acc[:], picked_ts[s][:], MULT)
+            finish(y[:], s, m)
+
+        A, B, C = PASS_ORDER
+        gather_words(A, 0)
+        gather_words(A, 1)
+        gather_ts(0)
+        ts_part = keep.tile([P, 4], F32, name="ts_part")
+        turned_ts = bank(7)
+        for i in range(4):
+            nc.tensor.transpose(turned_ts[:, i * P : (i + 1) * P], picked_ts[0][:, i * P : (i + 1) * P], ident[:])
+        nc.scalar.copy(ts_part[:], turned_ts[:, 0:NB:P])
+        gather_ts(1)
+        acc0 = [bank(i) for i in range(4)]
+        acc1 = [bank(4 + i) for i in range(4)]
+        mm_turned(acc0, A, 0)
+        for m in range(4):
+            mm_direct(acc1[m], A, 1, m)
+        gather_words(B, 0)
+        gather_words(B, 1)
+        mm_turned(acc0, B, 0)
+        for m in range(4):
+            mm_direct(acc1[m], B, 1, m)
+
+        w8_grouped = keep.tile([P, M, 4], BF16, name="w8_grouped", align_bytes=64)
+        nc.scalar.copy(w8_grouped[:], w8_raw[:].rearrange("p j n -> p n j"))
+        nc.vector.quantize_mx(out=w8_codes[:].bitcast(FP8X4), scales=w8_plane[:], in_=w8_grouped[:].rearrange("p n j -> p (n j)"))
+
+        gather_words(A, 2)
+        gather_words(B, 2)
+        gather_words(A, 3)
+        gather_words(C, 0)
+        mm_turned(acc0, C, 0)
+        gather_words(C, 1)
+        for m in range(4):
+            mm_direct(acc1[m], C, 1, m)
+        gather_words(C, 2)
+
+        yt = keep.tile([P, 4, M], F32, name="yt")
+        for i in range(4):
+            nc.scalar.activation(yt[:, i, :], acc0[i][:], COPY, scale=ts_part[:, i : i + 1])
+        for m in range(4):
+            scale_direct(acc1[m], 1, m)
+        for m in range(4):
+            back = bank(m)
+            for i in range(4):
+                nc.tensor.transpose(back[:, i * P : (i + 1) * P], yt[:, i, m * P : (m + 1) * P], ident[:])
+            finish(back[:], 0, m)
+
+        gather_ts(2, "picked0_1")
+        acc2 = [bank(4 + i) for i in range(4)]
+        for m in range(4):
+            for a in PASS_ORDER:
+                mm_direct(acc2[m], a, 2, m)
+        gather_words(B, 3, "picked0_0")
+        gather_words(C, 3)
+        gather_ts(3, "picked_ts1")
+        for m in range(4):
+            scale_direct(acc2[m], 2, m)
+        acc3 = [bank(i) for i in range(4)]
+        for m in range(4):
+            for a in PASS_ORDER:
+                mm_direct(acc3[m], a, 3, m)
+            scale_direct(acc3[m], 3, m)

@@ -41,39 +41,41 @@ def tile_list_tabts_gelu_kernel(tc, tab_words, tab_scales, w8, w4_words, w4_scal
         nc.sync.dma_start(scale_win[0:32, :], scale_rows[0:32, :])
         nc.sync.dma_start(scale_win[64:96, :], scale_rows[16:48, :])
         ts_rows = keep.tile([P, P], F32, name="ts_rows")
-        nc.sync.dma_start(ts_rows[:], ts[0:4, :].rearrange("a (c p) -> (a c) p", p=P))
+        nc.scalar.dma_start(ts_rows[:], ts[0:4, :].rearrange("a (c p) -> (a c) p", p=P))
 
-        table = {}
-        w8_raw = keep.tile([P, 4, M], F32, name="w8_raw")
-        for a in PASS_ORDER:
-            if a == 0:
-                nc.sync.dma_start(w8_raw[:], w8.rearrange("(p j) n -> p j n", j=4))
-            table[a] = keep.tile([P, T], I32, name="table%d" % a, align_bytes=64)
+        table = {a: keep.tile([P, T], I32, name="table%d" % a, align_bytes=64) for a in PASS_ORDER}
+
+        def load_table(a):
             nc.sync.dma_start(table[a][:], tab_words[a].rearrange("p t i -> p (t i)").bitcast(I32))
+
+        load_table(PASS_ORDER[0])
+        load_table(PASS_ORDER[1])
+        w4 = keep.tile([P, 2, 2 * M], U8, name="w4", align_bytes=64)
+        nc.sync.dma_start(w4[:].bitcast(I32), w4_words.rearrange("a p n -> p a n").bitcast(I32))
+        w8_raw = keep.tile([P, 4, M], F32, name="w8_raw")
+        nc.sync.dma_start(w8_raw[:], w8.rearrange("(p j) n -> p j n", j=4))
 
         warm = keep.tile([P, 2], F32, name="warm")
         nc.vector.memset(warm[:, 0:1], 0.0)
         nc.scalar.activation(warm[:, 1:2], warm[:, 0:1], GELU)
         nc.vector.memset(scale_win[32:64, :], 0)
         nc.vector.memset(scale_win[96:128, :], 0)
-        w4_plane = keep.tile([P, 2, M // 4], I32, name="w4_plane", align_bytes=64)
-        nc.vector.memset(w4_plane[:], 0)
         planes = keep.tile([P, 3, S // 4], I32, name="planes", align_bytes=64)
         nc.vector.memset(planes[:], 0)
+        w4_plane = keep.tile([P, 2, M // 4], I32, name="w4_plane", align_bytes=64)
+        nc.vector.memset(w4_plane[:], 0)
 
         ident = keep.tile([P, P], F32, name="ident")
         make_identity(nc, ident[:])
 
-        w4 = keep.tile([P, 2, 2 * M], U8, name="w4", align_bytes=64)
-        nc.gpsimd.dma_start(w4[:].bitcast(I32), w4_words.rearrange("a p n -> p a n").bitcast(I32))
         for q in range(4):
-            nc.gpsimd.dma_start(
+            nc.scalar.dma_start(
                 w4_plane[32 * q : 32 * q + 4, :, :],
                 w4_scales[:, 4 * q : 4 * q + 4, :].rearrange("a r n -> r a n").bitcast(I32),
             )
         bias = keep.tile([P, 4], F32, name="bias")
         with nc.allow_non_contiguous_dma(reason="one bias value a partition"):
-            nc.gpsimd.dma_start(bias[:], b.rearrange("(m p) -> p m", p=P))
+            nc.scalar.dma_start(bias[:], b.rearrange("(m p) -> p m", p=P))
 
         ts_cols = keep.tile([P, 32], F32, name="ts_cols")
         first = bank(0)
@@ -92,8 +94,9 @@ def tile_list_tabts_gelu_kernel(tc, tab_words, tab_scales, w8, w4_words, w4_scal
         for step, a in enumerate(PASS_ORDER):
             for q in range(4):
                 row = 16 * a + 4 * q if a < 2 else 64 + 16 + 4 * q
-                eng = nc.scalar if 4 * step + q < 6 else nc.gpsimd
+                eng = nc.scalar if 4 * step + q < 6 else nc.sync
                 eng.dma_start(planes[32 * q : 32 * q + 4, a, :], picked_scales[row : row + 4, :])
+        load_table(PASS_ORDER[2])
 
         picked = {}
         picked_ts = {}
@@ -198,9 +201,9 @@ def tile_list_tabts_gelu_kernel(tc, tab_words, tab_scales, w8, w4_words, w4_scal
                 mm_direct(acc2[m], a, 2, m)
         gather_words(B, 3, "picked0_0")
         gather_words(C, 3)
-        gather_ts(3, "picked_ts1")
         for m in range(4):
             scale_direct(acc2[m], 2, m)
+        gather_ts(3, "picked_ts1")
         acc3 = [bank(i) for i in range(4)]
         for m in range(4):
             for a in PASS_ORDER:

@@ -27,7 +27,7 @@ def tile_list_tabts_gelu_kernel(tc, tab_words, tab_scales, w8, w4_words, w4_scal
     nc = tc.nc
     with ExitStack() as ctx:
         keep = ctx.enter_context(tc.tile_pool(name="keep", bufs=1))
-        stage = ctx.enter_context(tc.tile_pool(name="stage", bufs=8))
+        stage = ctx.enter_context(tc.tile_pool(name="stage", bufs=12))
         psum = ctx.enter_context(tc.psum_pool(name="psum", bufs=1))
 
         def bank(i):
@@ -48,12 +48,18 @@ def tile_list_tabts_gelu_kernel(tc, tab_words, tab_scales, w8, w4_words, w4_scal
         def load_table(a):
             nc.sync.dma_start(table[a][:], tab_words[a].rearrange("p t i -> p (t i)").bitcast(I32))
 
-        load_table(PASS_ORDER[0])
-        load_table(PASS_ORDER[1])
         w4 = keep.tile([P, 2, 2 * M], U8, name="w4", align_bytes=64)
         nc.sync.dma_start(w4[:].bitcast(I32), w4_words.rearrange("a p n -> p a n").bitcast(I32))
+        load_table(PASS_ORDER[0])
+        w4_plane = keep.tile([P, 2, M // 4], I32, name="w4_plane", align_bytes=64)
+        nc.vector.memset(w4_plane[:], 0)
+        for q in range(4):
+            nc.sync.dma_start(
+                w4_plane[32 * q : 32 * q + 4, :, :],
+                w4_scales[:, 4 * q : 4 * q + 4, :].rearrange("a r n -> r a n").bitcast(I32),
+            )
+        load_table(PASS_ORDER[1])
         w8_raw = keep.tile([P, 4, M], F32, name="w8_raw")
-        nc.sync.dma_start(w8_raw[:], w8.rearrange("(p j) n -> p j n", j=4))
 
         warm = keep.tile([P, 2], F32, name="warm")
         nc.vector.memset(warm[:, 0:1], 0.0)
@@ -61,18 +67,11 @@ def tile_list_tabts_gelu_kernel(tc, tab_words, tab_scales, w8, w4_words, w4_scal
         nc.vector.memset(scale_win[32:64, :], 0)
         nc.vector.memset(scale_win[96:128, :], 0)
         planes = keep.tile([P, 3, S // 4], I32, name="planes", align_bytes=64)
-        nc.vector.memset(planes[:], 0)
-        w4_plane = keep.tile([P, 2, M // 4], I32, name="w4_plane", align_bytes=64)
-        nc.vector.memset(w4_plane[:], 0)
 
         ident = keep.tile([P, P], F32, name="ident")
         make_identity(nc, ident[:])
+        nc.gpsimd.memset(planes[:], 0)
 
-        for q in range(4):
-            nc.scalar.dma_start(
-                w4_plane[32 * q : 32 * q + 4, :, :],
-                w4_scales[:, 4 * q : 4 * q + 4, :].rearrange("a r n -> r a n").bitcast(I32),
-            )
         bias = keep.tile([P, 4], F32, name="bias")
         with nc.allow_non_contiguous_dma(reason="one bias value a partition"):
             nc.scalar.dma_start(bias[:], b.rearrange("(m p) -> p m", p=P))
@@ -91,12 +90,19 @@ def tile_list_tabts_gelu_kernel(tc, tab_words, tab_scales, w8, w4_words, w4_scal
 
         picked_scales = keep.tile([P, S // 4], I32, name="picked_scales", align_bytes=64)
         nc.vector.tensor_copy(picked_scales[:].bitcast(U8), scale_win[:].bitcast(U8).indirect(offsets[:]))
-        for step, a in enumerate(PASS_ORDER):
-            for q in range(4):
+
+        moves = [(a, q) for a in PASS_ORDER for q in range(4)]
+
+        def move_scales(some):
+            for a, q in some:
                 row = 16 * a + 4 * q if a < 2 else 64 + 16 + 4 * q
-                eng = nc.scalar if 4 * step + q < 6 else nc.sync
-                eng.dma_start(planes[32 * q : 32 * q + 4, a, :], picked_scales[row : row + 4, :])
+                nc.sync.dma_start(planes[32 * q : 32 * q + 4, a, :], picked_scales[row : row + 4, :])
+
+        move_scales(moves[:4])
+        nc.sync.dma_start(w8_raw[:], w8.rearrange("(p j) n -> p j n", j=4))
+        move_scales(moves[4:8])
         load_table(PASS_ORDER[2])
+        move_scales(moves[8:])
 
         picked = {}
         picked_ts = {}
@@ -138,74 +144,91 @@ def tile_list_tabts_gelu_kernel(tc, tab_words, tab_scales, w8, w4_words, w4_scal
         def mm_direct(acc, a, s, m):
             mm(acc, a, weights(a, m * P, (m + 1) * P), tokens(a, s * NB, (s + 1) * NB))
 
-        def finish(src, s, m):
-            res = stage.tile([P, NB], F32, name="res")
-            nc.scalar.activation(res[:], src, GELU, bias=bias[:, m : m + 1])
-            nc.sync.dma_start(out[m * P : (m + 1) * P, s * NB : (s + 1) * NB], res[:])
+        def store(res, s, m, c0, c1):
+            nc.sync.dma_start(out[m * P : (m + 1) * P, s * NB + c0 : s * NB + c1], res[:, c0:c1])
 
-        def scale_direct(acc, s, m):
+        def finish_direct(acc, s, m, pieces=1):
             y = stage.tile([P, NB], F32, name="y")
-            nc.vector.tensor_tensor(y[:], acc[:], picked_ts[s][:], MULT)
-            finish(y[:], s, m)
+            res = stage.tile([P, NB], F32, name="res")
+            width = NB // pieces
+            for c0 in range(0, NB, width):
+                cols = slice(c0, c0 + width)
+                nc.vector.tensor_tensor(y[:, cols], acc[:, cols], picked_ts[s][:, cols], MULT)
+                nc.scalar.activation(res[:, cols], y[:, cols], GELU, bias=bias[:, m : m + 1])
+                store(res, s, m, c0, c0 + width)
+
+        def turn_ts(s, free_bank):
+            part = keep.tile([P, 4], F32, name="ts_part%d" % s)
+            turned = bank(free_bank)
+            for i in range(4):
+                nc.tensor.transpose(turned[:, i * P : (i + 1) * P], picked_ts[s][:, i * P : (i + 1) * P], ident[:])
+            nc.scalar.copy(part[:], turned[:, 0:NB:P])
+            return part
+
+        def finish_turned(accs, s, part, banks):
+            yt = keep.tile([P, 4, M], F32, name="yt%d" % s, align_bytes=64)
+            results = [stage.tile([P, NB], F32, name="res") for m in range(4)]
+            for i in range(4):
+                nc.scalar.activation(yt[:, i, :], accs[i][:], COPY, scale=part[:, i : i + 1])
+            for half in range(2):
+                for pair in range(2):
+                    back = bank(banks[2 * half + pair])
+                    for u in range(4):
+                        m, i = 2 * pair + u // 2, 2 * half + u % 2
+                        nc.tensor.transpose(back[:, u * P : (u + 1) * P], yt[:, i, m * P : (m + 1) * P], ident[:])
+                    for m in (2 * pair, 2 * pair + 1):
+                        nc.scalar.activation(
+                            results[m][:, half * 2 * P : (half + 1) * 2 * P],
+                            back[:, (m % 2) * 2 * P : (m % 2 + 1) * 2 * P],
+                            GELU,
+                            bias=bias[:, m : m + 1],
+                        )
+                        if half == 1:
+                            store(results[m], s, m, 0, NB)
+
+        def multiply_direct(accs, s, passes):
+            for m in range(4):
+                for a in passes:
+                    mm_direct(accs[m], a, s, m)
 
         A, B, C = PASS_ORDER
         gather_words(A, 0)
         gather_words(A, 1)
         gather_ts(0)
-        ts_part = keep.tile([P, 4], F32, name="ts_part")
-        turned_ts = bank(7)
-        for i in range(4):
-            nc.tensor.transpose(turned_ts[:, i * P : (i + 1) * P], picked_ts[0][:, i * P : (i + 1) * P], ident[:])
-        nc.scalar.copy(ts_part[:], turned_ts[:, 0:NB:P])
+        part0 = turn_ts(0, 7)
         gather_ts(1)
         acc0 = [bank(i) for i in range(4)]
         acc1 = [bank(4 + i) for i in range(4)]
         mm_turned(acc0, A, 0)
-        for m in range(4):
-            mm_direct(acc1[m], A, 1, m)
+        multiply_direct(acc1, 1, (A,))
         gather_words(B, 0)
         gather_words(B, 1)
         mm_turned(acc0, B, 0)
-        for m in range(4):
-            mm_direct(acc1[m], B, 1, m)
-
+        multiply_direct(acc1, 1, (B,))
         w8_grouped = keep.tile([P, M, 4], BF16, name="w8_grouped", align_bytes=64)
         nc.scalar.copy(w8_grouped[:], w8_raw[:].rearrange("p j n -> p n j"))
         nc.vector.quantize_mx(out=w8_codes[:].bitcast(FP8X4), scales=w8_plane[:], in_=w8_grouped[:].rearrange("p n j -> p (n j)"))
-
-        gather_words(A, 2)
-        gather_words(B, 2)
-        gather_words(A, 3)
         gather_words(C, 0)
         mm_turned(acc0, C, 0)
         gather_words(C, 1)
-        for m in range(4):
-            mm_direct(acc1[m], C, 1, m)
+        multiply_direct(acc1, 1, (C,))
+        gather_words(A, 2)
+        gather_words(B, 2)
+        gather_words(A, 3)
         gather_words(C, 2)
 
-        yt = keep.tile([P, 4, M], F32, name="yt")
-        for i in range(4):
-            nc.scalar.activation(yt[:, i, :], acc0[i][:], COPY, scale=ts_part[:, i : i + 1])
+        finish_turned(acc0, 0, part0, (0, 1, 2, 3))
         for m in range(4):
-            scale_direct(acc1[m], 1, m)
-        for m in range(4):
-            back = bank(m)
-            for i in range(4):
-                nc.tensor.transpose(back[:, i * P : (i + 1) * P], yt[:, i, m * P : (m + 1) * P], ident[:])
-            finish(back[:], 0, m)
-
-        gather_ts(2, "picked0_1")
+            finish_direct(acc1[m], 1, m)
         acc2 = [bank(4 + i) for i in range(4)]
-        for m in range(4):
-            for a in PASS_ORDER:
-                mm_direct(acc2[m], a, 2, m)
+        multiply_direct(acc2, 2, PASS_ORDER)
+        gather_ts(2, "picked0_1")
         gather_words(B, 3, "picked0_0")
         gather_words(C, 3)
         for m in range(4):
-            scale_direct(acc2[m], 2, m)
-        gather_ts(3, "picked_ts1")
+            finish_direct(acc2[m], 2, m)
         acc3 = [bank(i) for i in range(4)]
+        multiply_direct(acc3, 3, PASS_ORDER)
+        gather_ts(3, "picked_ts1")
         for m in range(4):
-            for a in PASS_ORDER:
-                mm_direct(acc3[m], a, 3, m)
-            scale_direct(acc3[m], 3, m)
+            finish_direct(acc3[m], 3, m, 2 if m == 3 else 1)

@@ -25,6 +25,7 @@ PASS_ORDER = (1, 2, 0)
 
 def tile_list_tabts_gelu_kernel(tc, tab_words, tab_scales, w8, w4_words, w4_scales, ts, b, offs, out):
     nc = tc.nc
+    A, B, C = PASS_ORDER
     with ExitStack() as ctx:
         keep = ctx.enter_context(tc.tile_pool(name="keep", bufs=1))
         stage = ctx.enter_context(tc.tile_pool(name="stage", bufs=12))
@@ -36,21 +37,26 @@ def tile_list_tabts_gelu_kernel(tc, tab_words, tab_scales, w8, w4_words, w4_scal
         offsets = keep.tile([P, S // 16], U16, name="offsets")
         nc.sync.dma_start(offsets[:], offs)
 
-        scale_rows = tab_scales.rearrange("a q t -> (a q) t").bitcast(I32)
         scale_win = keep.tile([P, T // 4], I32, name="scale_win", align_bytes=64)
-        nc.sync.dma_start(scale_win[0:32, :], scale_rows[0:32, :])
-        nc.sync.dma_start(scale_win[64:96, :], scale_rows[16:48, :])
+        nc.vector.memset(scale_win[64:128, :], 0)
+        nc.vector.memset(scale_win[32:64, :], 0)
+        nc.sync.dma_start(scale_win[0:32, :], tab_scales[1:3].rearrange("a q t -> q a t").bitcast(I32))
         ts_rows = keep.tile([P, P], F32, name="ts_rows")
-        nc.scalar.dma_start(ts_rows[:], ts[0:4, :].rearrange("a (c p) -> (a c) p", p=P))
+        nc.scalar.dma_start(ts_rows[0:32, :], ts[0].rearrange("(c p) -> c p", p=P))
+        nc.sync.dma_start(scale_win[64:80, :], tab_scales[0].bitcast(I32))
+        nc.vector.memset(ts_rows[32:64, :], 0.0)
+        nc.vector.memset(ts_rows[64:128, :], 0.0)
+        b_rows = keep.tile([P, P], F32, name="b_rows")
+        nc.vector.memset(b_rows[:], 0.0)
 
         table = {a: keep.tile([P, T], I32, name="table%d" % a, align_bytes=64) for a in PASS_ORDER}
 
         def load_table(a):
             nc.sync.dma_start(table[a][:], tab_words[a].rearrange("p t i -> p (t i)").bitcast(I32))
 
+        load_table(A)
         w4 = keep.tile([P, 2, 2 * M], U8, name="w4", align_bytes=64)
         nc.sync.dma_start(w4[:].bitcast(I32), w4_words.rearrange("a p n -> p a n").bitcast(I32))
-        load_table(PASS_ORDER[0])
         w4_plane = keep.tile([P, 2, M // 4], I32, name="w4_plane", align_bytes=64)
         nc.vector.memset(w4_plane[:], 0)
         for q in range(4):
@@ -58,23 +64,17 @@ def tile_list_tabts_gelu_kernel(tc, tab_words, tab_scales, w8, w4_words, w4_scal
                 w4_plane[32 * q : 32 * q + 4, :, :],
                 w4_scales[:, 4 * q : 4 * q + 4, :].rearrange("a r n -> r a n").bitcast(I32),
             )
-        load_table(PASS_ORDER[1])
-        w8_raw = keep.tile([P, 4, M], F32, name="w8_raw")
+        nc.sync.dma_start(b_rows[0:4, :], b.rearrange("(m p) -> m p", p=P))
+        load_table(B)
 
         warm = keep.tile([P, 2], F32, name="warm")
         nc.vector.memset(warm[:, 0:1], 0.0)
         nc.scalar.activation(warm[:, 1:2], warm[:, 0:1], GELU)
-        nc.vector.memset(scale_win[32:64, :], 0)
-        nc.vector.memset(scale_win[96:128, :], 0)
-        planes = keep.tile([P, 3, S // 4], I32, name="planes", align_bytes=64)
+        planes = keep.tile([P, 2, S // 4], I32, name="planes", align_bytes=64)
 
         ident = keep.tile([P, P], F32, name="ident")
         make_identity(nc, ident[:])
         nc.gpsimd.memset(planes[:], 0)
-
-        bias = keep.tile([P, 4], F32, name="bias")
-        with nc.allow_non_contiguous_dma(reason="one bias value a partition"):
-            nc.scalar.dma_start(bias[:], b.rearrange("(m p) -> p m", p=P))
 
         ts_cols = keep.tile([P, 32], F32, name="ts_cols")
         first = bank(0)
@@ -87,22 +87,21 @@ def tile_list_tabts_gelu_kernel(tc, tab_words, tab_scales, w8, w4_words, w4_scal
                 col = 4 * g + c
                 nc.tensor.transpose(spread[:, c * P : (c + 1) * P], ts_cols[:, col : col + 1].to_broadcast([P, P]), ident[:])
             nc.scalar.copy(ts_win[:, g * NB : (g + 1) * NB], spread[:])
+        bias = keep.tile([P, 4], F32, name="bias")
+        b_turned = bank(5)
+        nc.tensor.transpose(b_turned[:, 0:P], b_rows[:], ident[:])
+        nc.scalar.copy(bias[:], b_turned[:, 0:4])
 
         picked_scales = keep.tile([P, S // 4], I32, name="picked_scales", align_bytes=64)
         nc.vector.tensor_copy(picked_scales[:].bitcast(U8), scale_win[:].bitcast(U8).indirect(offsets[:]))
 
-        moves = [(a, q) for a in PASS_ORDER for q in range(4)]
-
-        def move_scales(some):
-            for a, q in some:
-                row = 16 * a + 4 * q if a < 2 else 64 + 16 + 4 * q
-                nc.sync.dma_start(planes[32 * q : 32 * q + 4, a, :], picked_scales[row : row + 4, :])
-
-        move_scales(moves[:4])
+        for q in range(4):
+            nc.sync.dma_start(planes[32 * q : 32 * q + 4, :, :], picked_scales[8 * q : 8 * q + 8, :])
+        w8_raw = keep.tile([P, 4, M], F32, name="w8_raw")
         nc.sync.dma_start(w8_raw[:], w8.rearrange("(p j) n -> p j n", j=4))
-        move_scales(moves[4:8])
-        load_table(PASS_ORDER[2])
-        move_scales(moves[8:])
+        for q in range(4):
+            nc.sync.dma_start(planes[32 * q + 4 : 32 * q + 8, 1, :], picked_scales[64 + 4 * q : 64 + 4 * q + 4, :])
+        load_table(C)
 
         picked = {}
         picked_ts = {}
@@ -112,14 +111,12 @@ def tile_list_tabts_gelu_kernel(tc, tab_words, tab_scales, w8, w4_words, w4_scal
         def cut(s):
             return offsets[:, s * 32 : (s + 1) * 32]
 
-        def gather_words(a, s, slot=None):
-            name = "picked%d_%d" % (a, s)
-            picked[a, s] = keep.tile([P, NB], U32, name=name, tag=slot or name, align_bytes=64)
+        def gather_words(a, s):
+            picked[a, s] = keep.tile([P, NB], U32, name="picked%d_%d" % (a, s), align_bytes=64)
             nc.vector.tensor_copy(picked[a, s][:], table[a][:].bitcast(U32).indirect(cut(s)))
 
-        def gather_ts(s, slot=None):
-            name = "picked_ts%d" % s
-            picked_ts[s] = keep.tile([P, NB], F32, name=name, tag=slot or name, align_bytes=64)
+        def gather_ts(s, slot):
+            picked_ts[s] = keep.tile([P, NB], F32, name="picked_ts%d" % s, tag=slot, align_bytes=64)
             nc.vector.tensor_copy(picked_ts[s][:], ts_win[:].indirect(cut(s)))
 
         def weights(a, n0, n1):
@@ -128,12 +125,15 @@ def tile_list_tabts_gelu_kernel(tc, tab_words, tab_scales, w8, w4_words, w4_scal
             return w4[:, a - 1, 2 * n0 : 2 * n1].bitcast(FP4X4), w4_plane[:, a - 1, :].bitcast(U8)[:, n0:n1]
 
         def tokens(a, j0, j1):
-            return picked[a, j0 // NB][:, j0 % NB : j0 % NB + j1 - j0].bitcast(FP8X4), planes[:, a, :].bitcast(U8)[:, j0:j1]
+            codes = picked[a, j0 // NB][:, j0 % NB : j0 % NB + j1 - j0].bitcast(FP8X4)
+            if a == 0:
+                return codes, planes[4:P, 1, :].bitcast(U8)[:, j0:j1]
+            return codes, planes[:, a - 1, :].bitcast(U8)[:, j0:j1]
 
         def mm(acc, a, lhs, rhs):
             nc.tensor.matmul_mx(
                 out=acc[:], lhsT=lhs[0], lhsT_scale=lhs[1], rhs=rhs[0], rhs_scale=rhs[1],
-                start=(a == PASS_ORDER[0]), stop=(a == PASS_ORDER[-1]),
+                start=(a == A), stop=(a == C),
             )
 
         def mm_turned(accs, a, s):
@@ -141,8 +141,10 @@ def tile_list_tabts_gelu_kernel(tc, tab_words, tab_scales, w8, w4_words, w4_scal
                 j0 = s * NB + i * P
                 mm(accs[i], a, tokens(a, j0, j0 + P), weights(a, 0, M))
 
-        def mm_direct(acc, a, s, m):
-            mm(acc, a, weights(a, m * P, (m + 1) * P), tokens(a, s * NB, (s + 1) * NB))
+        def multiply_direct(accs, s, passes):
+            for m in range(4):
+                for a in passes:
+                    mm(accs[m], a, weights(a, m * P, (m + 1) * P), tokens(a, s * NB, (s + 1) * NB))
 
         def store(res, s, m, c0, c1):
             nc.sync.dma_start(out[m * P : (m + 1) * P, s * NB + c0 : s * NB + c1], res[:, c0:c1])
@@ -167,68 +169,47 @@ def tile_list_tabts_gelu_kernel(tc, tab_words, tab_scales, w8, w4_words, w4_scal
 
         def finish_turned(accs, s, part, banks):
             yt = keep.tile([P, 4, M], F32, name="yt%d" % s, align_bytes=64)
-            results = [stage.tile([P, NB], F32, name="res") for m in range(4)]
             for i in range(4):
                 nc.scalar.activation(yt[:, i, :], accs[i][:], COPY, scale=part[:, i : i + 1])
-            for half in range(2):
-                for pair in range(2):
-                    back = bank(banks[2 * half + pair])
-                    for u in range(4):
-                        m, i = 2 * pair + u // 2, 2 * half + u % 2
-                        nc.tensor.transpose(back[:, u * P : (u + 1) * P], yt[:, i, m * P : (m + 1) * P], ident[:])
-                    for m in (2 * pair, 2 * pair + 1):
-                        nc.scalar.activation(
-                            results[m][:, half * 2 * P : (half + 1) * 2 * P],
-                            back[:, (m % 2) * 2 * P : (m % 2 + 1) * 2 * P],
-                            GELU,
-                            bias=bias[:, m : m + 1],
-                        )
-                        if half == 1:
-                            store(results[m], s, m, 0, NB)
-
-        def multiply_direct(accs, s, passes):
             for m in range(4):
-                for a in passes:
-                    mm_direct(accs[m], a, s, m)
+                back = bank(banks[m])
+                for i in range(4):
+                    nc.tensor.transpose(back[:, i * P : (i + 1) * P], yt[:, i, m * P : (m + 1) * P], ident[:])
+                res = stage.tile([P, NB], F32, name="res")
+                nc.scalar.activation(res[:], back[:], GELU, bias=bias[:, m : m + 1])
+                store(res, s, m, 0, NB)
 
-        A, B, C = PASS_ORDER
-        gather_words(A, 0)
-        gather_words(A, 1)
-        gather_ts(0)
+        for s in range(4):
+            gather_words(A, s)
+        gather_ts(0, "ts_turned")
         part0 = turn_ts(0, 7)
-        gather_ts(1)
+        gather_ts(1, "ts_direct")
         acc0 = [bank(i) for i in range(4)]
         acc1 = [bank(4 + i) for i in range(4)]
         mm_turned(acc0, A, 0)
         multiply_direct(acc1, 1, (A,))
-        gather_words(B, 0)
-        gather_words(B, 1)
+        for s in (2, 3, 0, 1):
+            gather_words(B, s)
         mm_turned(acc0, B, 0)
         multiply_direct(acc1, 1, (B,))
         w8_grouped = keep.tile([P, M, 4], BF16, name="w8_grouped", align_bytes=64)
         nc.scalar.copy(w8_grouped[:], w8_raw[:].rearrange("p j n -> p n j"))
         nc.vector.quantize_mx(out=w8_codes[:].bitcast(FP8X4), scales=w8_plane[:], in_=w8_grouped[:].rearrange("p n j -> p (n j)"))
-        gather_words(C, 0)
+        for s in range(4):
+            gather_words(C, s)
         mm_turned(acc0, C, 0)
-        gather_words(C, 1)
         multiply_direct(acc1, 1, (C,))
-        gather_words(A, 2)
-        gather_words(B, 2)
-        gather_words(A, 3)
-        gather_words(C, 2)
 
         finish_turned(acc0, 0, part0, (0, 1, 2, 3))
         for m in range(4):
             finish_direct(acc1[m], 1, m)
         acc2 = [bank(4 + i) for i in range(4)]
         multiply_direct(acc2, 2, PASS_ORDER)
-        gather_ts(2, "picked0_1")
-        gather_words(B, 3, "picked0_0")
-        gather_words(C, 3)
+        gather_ts(2, "ts_direct")
         for m in range(4):
             finish_direct(acc2[m], 2, m)
         acc3 = [bank(i) for i in range(4)]
         multiply_direct(acc3, 3, PASS_ORDER)
-        gather_ts(3, "picked_ts1")
+        gather_ts(3, "ts_direct")
         for m in range(4):
             finish_direct(acc3[m], 3, m, 2 if m == 3 else 1)

@@ -20,6 +20,7 @@ MULT = mybir.AluOpType.mult
 
 P = 128
 NB = 512
+HALF = S // 2
 PASS_ORDER = (1, 2, 0)
 
 
@@ -38,9 +39,9 @@ def tile_list_tabts_gelu_kernel(tc, tab_words, tab_scales, w8, w4_words, w4_scal
         nc.sync.dma_start(offsets[:], offs)
 
         scale_win = keep.tile([P, T // 4], I32, name="scale_win", align_bytes=64)
-        nc.vector.memset(scale_win[64:128, :], 0)
+        nc.gpsimd.memset(scale_win[64:128, :], 0)
         nc.vector.memset(scale_win[32:64, :], 0)
-        nc.sync.dma_start(scale_win[0:32, :], tab_scales[1:3].rearrange("a q t -> q a t").bitcast(I32))
+        nc.sync.dma_start(scale_win[0:32, :], tab_scales[1:3].rearrange("a q t -> (a q) t").bitcast(I32))
         ts_rows = keep.tile([P, P], F32, name="ts_rows")
         nc.scalar.dma_start(ts_rows[0:32, :], ts[0].rearrange("(c p) -> c p", p=P))
         nc.sync.dma_start(scale_win[64:80, :], tab_scales[0].bitcast(I32))
@@ -59,22 +60,20 @@ def tile_list_tabts_gelu_kernel(tc, tab_words, tab_scales, w8, w4_words, w4_scal
         nc.sync.dma_start(w4[:].bitcast(I32), w4_words.rearrange("a p n -> p a n").bitcast(I32))
         w4_plane = keep.tile([P, 2, M // 4], I32, name="w4_plane", align_bytes=64)
         nc.vector.memset(w4_plane[:], 0)
-        for q in range(4):
-            nc.sync.dma_start(
-                w4_plane[32 * q : 32 * q + 4, :, :],
-                w4_scales[:, 4 * q : 4 * q + 4, :].rearrange("a r n -> r a n").bitcast(I32),
-            )
+        for r in range(4):
+            nc.sync.dma_start(w4_plane[r:P:32, :, :], w4_scales[:, r:16:4, :].rearrange("a q n -> q a n").bitcast(I32))
         nc.sync.dma_start(b_rows[0:4, :], b.rearrange("(m p) -> m p", p=P))
         load_table(B)
 
         warm = keep.tile([P, 2], F32, name="warm")
         nc.vector.memset(warm[:, 0:1], 0.0)
         nc.scalar.activation(warm[:, 1:2], warm[:, 0:1], GELU)
-        planes = keep.tile([P, 2, S // 4], I32, name="planes", align_bytes=64)
+        planes = [keep.tile([P, 2, HALF // 4], I32, name="planes%d" % h, align_bytes=64) for h in range(2)]
+        for h in range(2):
+            nc.vector.memset(planes[h][:], 0)
 
         ident = keep.tile([P, P], F32, name="ident")
         make_identity(nc, ident[:])
-        nc.gpsimd.memset(planes[:], 0)
 
         ts_cols = keep.tile([P, 32], F32, name="ts_cols")
         first = bank(0)
@@ -95,13 +94,25 @@ def tile_list_tabts_gelu_kernel(tc, tab_words, tab_scales, w8, w4_words, w4_scal
         picked_scales = keep.tile([P, S // 4], I32, name="picked_scales", align_bytes=64)
         nc.vector.tensor_copy(picked_scales[:].bitcast(U8), scale_win[:].bitcast(U8).indirect(offsets[:]))
 
-        for q in range(4):
-            nc.sync.dma_start(planes[32 * q : 32 * q + 4, :, :], picked_scales[8 * q : 8 * q + 8, :])
+        first_row = {1: 0, 2: 16, 0: 64}
+        plane_row = {1: 0, 2: 0, 0: 4}
+        plane_col = {1: 0, 2: 1, 0: 1}
+
+        def move_scales(h, rows):
+            words = slice(h * HALF // 4, (h + 1) * HALF // 4)
+            for a, r in rows:
+                nc.sync.dma_start(
+                    planes[h][plane_row[a] + r : P : 32, plane_col[a], :],
+                    picked_scales[first_row[a] + r : first_row[a] + 16 : 4, words],
+                )
+
+        rows = [(a, r) for a in PASS_ORDER for r in range(4)]
+        move_scales(0, rows[:6])
         w8_raw = keep.tile([P, 4, M], F32, name="w8_raw")
         nc.sync.dma_start(w8_raw[:], w8.rearrange("(p j) n -> p j n", j=4))
-        for q in range(4):
-            nc.sync.dma_start(planes[32 * q + 4 : 32 * q + 8, 1, :], picked_scales[64 + 4 * q : 64 + 4 * q + 4, :])
+        move_scales(0, rows[6:])
         load_table(C)
+        move_scales(1, rows)
 
         picked = {}
         picked_ts = {}
@@ -126,9 +137,8 @@ def tile_list_tabts_gelu_kernel(tc, tab_words, tab_scales, w8, w4_words, w4_scal
 
         def tokens(a, j0, j1):
             codes = picked[a, j0 // NB][:, j0 % NB : j0 % NB + j1 - j0].bitcast(FP8X4)
-            if a == 0:
-                return codes, planes[4:P, 1, :].bitcast(U8)[:, j0:j1]
-            return codes, planes[:, a - 1, :].bitcast(U8)[:, j0:j1]
+            plane = planes[j0 // HALF][plane_row[a] : P, plane_col[a], :].bitcast(U8)
+            return codes, plane[:, j0 % HALF : j0 % HALF + j1 - j0]
 
         def mm(acc, a, lhs, rhs):
             nc.tensor.matmul_mx(

@@ -15,7 +15,6 @@ U8 = mybir.dt.uint8
 FP8X4 = mybir.dt.float8_e4m3fn_x4
 FP4X4 = mybir.dt.float4_e2m1fn_x4
 GELU = mybir.ActivationFunctionType.Gelu_apprx_tanh
-COPY = mybir.ActivationFunctionType.Copy
 MULT = mybir.AluOpType.mult
 
 P = 128
@@ -115,111 +114,70 @@ def tile_list_tabts_gelu_kernel(tc, tab_words, tab_scales, w8, w4_words, w4_scal
         move_scales(1, rows)
 
         picked = {}
-        picked_ts = {}
         w8_codes = keep.tile([P, M], U32, name="w8_codes", align_bytes=64)
         w8_plane = keep.tile([P, M], U8, name="w8_plane", align_bytes=64)
 
-        def cut(s):
-            return offsets[:, s * 32 : (s + 1) * 32]
+        def gather_words(a, s0, s1, slot=None):
+            name = "picked%d_%d" % (a, s0)
+            words = keep.tile([P, (s1 - s0) * NB], U32, name=name, tag=slot or name, align_bytes=64)
+            nc.vector.tensor_copy(words[:], table[a][:].bitcast(U32).indirect(offsets[:, s0 * 32 : s1 * 32]))
+            for s in range(s0, s1):
+                picked[a, s] = words[:, (s - s0) * NB : (s - s0 + 1) * NB]
 
-        def gather_words(a, s):
-            picked[a, s] = keep.tile([P, NB], U32, name="picked%d_%d" % (a, s), align_bytes=64)
-            nc.vector.tensor_copy(picked[a, s][:], table[a][:].bitcast(U32).indirect(cut(s)))
-
-        def gather_ts(s, slot):
-            picked_ts[s] = keep.tile([P, NB], F32, name="picked_ts%d" % s, tag=slot, align_bytes=64)
-            nc.vector.tensor_copy(picked_ts[s][:], ts_win[:].indirect(cut(s)))
-
-        def weights(a, n0, n1):
+        def weights(a, m):
+            n0, n1 = m * P, (m + 1) * P
             if a == 0:
                 return w8_codes[:, n0:n1].bitcast(FP8X4), w8_plane[:, n0:n1]
             return w4[:, a - 1, 2 * n0 : 2 * n1].bitcast(FP4X4), w4_plane[:, a - 1, :].bitcast(U8)[:, n0:n1]
 
-        def tokens(a, j0, j1):
-            codes = picked[a, j0 // NB][:, j0 % NB : j0 % NB + j1 - j0].bitcast(FP8X4)
-            plane = planes[j0 // HALF][plane_row[a] : P, plane_col[a], :].bitcast(U8)
-            return codes, plane[:, j0 % HALF : j0 % HALF + j1 - j0]
-
-        def mm(acc, a, lhs, rhs):
-            nc.tensor.matmul_mx(
-                out=acc[:], lhsT=lhs[0], lhsT_scale=lhs[1], rhs=rhs[0], rhs_scale=rhs[1],
-                start=(a == A), stop=(a == C),
-            )
-
-        def mm_turned(accs, a, s):
-            for i in range(4):
-                j0 = s * NB + i * P
-                mm(accs[i], a, tokens(a, j0, j0 + P), weights(a, 0, M))
-
-        def multiply_direct(accs, s, passes):
+        def multiply(accs, s, passes):
             for m in range(4):
                 for a in passes:
-                    mm(accs[m], a, weights(a, m * P, (m + 1) * P), tokens(a, s * NB, (s + 1) * NB))
+                    codes, scales = weights(a, m)
+                    plane = planes[s // 2][plane_row[a] : P, plane_col[a], :].bitcast(U8)
+                    nc.tensor.matmul_mx(
+                        out=accs[m][:], lhsT=codes, lhsT_scale=scales,
+                        rhs=picked[a, s].bitcast(FP8X4), rhs_scale=plane[:, (s % 2) * NB : (s % 2 + 1) * NB],
+                        start=(a == A), stop=(a == C),
+                    )
 
-        def store(res, s, m, c0, c1):
-            nc.sync.dma_start(out[m * P : (m + 1) * P, s * NB + c0 : s * NB + c1], res[:, c0:c1])
-
-        def finish_direct(acc, s, m, pieces=1):
-            y = stage.tile([P, NB], F32, name="y")
-            res = stage.tile([P, NB], F32, name="res")
-            width = NB // pieces
-            for c0 in range(0, NB, width):
-                cols = slice(c0, c0 + width)
-                nc.vector.tensor_tensor(y[:, cols], acc[:, cols], picked_ts[s][:, cols], MULT)
-                nc.scalar.activation(res[:, cols], y[:, cols], GELU, bias=bias[:, m : m + 1])
-                store(res, s, m, c0, c0 + width)
-
-        def turn_ts(s, free_bank):
-            part = keep.tile([P, 4], F32, name="ts_part%d" % s)
-            turned = bank(free_bank)
-            for i in range(4):
-                nc.tensor.transpose(turned[:, i * P : (i + 1) * P], picked_ts[s][:, i * P : (i + 1) * P], ident[:])
-            nc.scalar.copy(part[:], turned[:, 0:NB:P])
-            return part
-
-        def finish_turned(accs, s, part, banks):
-            yt = keep.tile([P, 4, M], F32, name="yt%d" % s, align_bytes=64)
-            for i in range(4):
-                nc.scalar.activation(yt[:, i, :], accs[i][:], COPY, scale=part[:, i : i + 1])
+        def finish(accs, s):
             for m in range(4):
-                back = bank(banks[m])
-                for i in range(4):
-                    nc.tensor.transpose(back[:, i * P : (i + 1) * P], yt[:, i, m * P : (m + 1) * P], ident[:])
+                y = stage.tile([P, NB], F32, name="y")
                 res = stage.tile([P, NB], F32, name="res")
-                nc.scalar.activation(res[:], back[:], GELU, bias=bias[:, m : m + 1])
-                store(res, s, m, 0, NB)
+                width = NB // 2 if (s, m) == (3, 3) else NB
+                for c0 in range(0, NB, width):
+                    cols = slice(c0, c0 + width)
+                    tokens = slice(s * NB + c0, s * NB + c0 + width)
+                    nc.vector.tensor_tensor(y[:, cols], accs[m][:, cols], picked_ts[:, tokens], MULT)
+                    nc.scalar.activation(res[:, cols], y[:, cols], GELU, bias=bias[:, m : m + 1])
+                    nc.sync.dma_start(out[m * P : (m + 1) * P, tokens], res[:, cols])
 
-        for s in range(4):
-            gather_words(A, s)
-        gather_ts(0, "ts_turned")
-        part0 = turn_ts(0, 7)
-        gather_ts(1, "ts_direct")
+        gather_words(A, 0, 4)
+        picked_ts = keep.tile([P, S], F32, name="picked_ts", align_bytes=64)
+        nc.vector.tensor_copy(picked_ts[:], ts_win[:].indirect(offsets[:]))
         acc0 = [bank(i) for i in range(4)]
         acc1 = [bank(4 + i) for i in range(4)]
-        mm_turned(acc0, A, 0)
-        multiply_direct(acc1, 1, (A,))
-        for s in (2, 3, 0, 1):
-            gather_words(B, s)
-        mm_turned(acc0, B, 0)
-        multiply_direct(acc1, 1, (B,))
+        multiply(acc0, 0, (A,))
+        multiply(acc1, 1, (A,))
+        gather_words(B, 0, 2)
+        gather_words(B, 2, 4)
+        multiply(acc0, 0, (B,))
+        multiply(acc1, 1, (B,))
         w8_grouped = keep.tile([P, M, 4], BF16, name="w8_grouped", align_bytes=64)
         nc.scalar.copy(w8_grouped[:], w8_raw[:].rearrange("p j n -> p n j"))
         nc.vector.quantize_mx(out=w8_codes[:].bitcast(FP8X4), scales=w8_plane[:], in_=w8_grouped[:].rearrange("p n j -> p (n j)"))
-        for s in range(4):
-            gather_words(C, s)
-        mm_turned(acc0, C, 0)
-        multiply_direct(acc1, 1, (C,))
-
-        finish_turned(acc0, 0, part0, (0, 1, 2, 3))
-        for m in range(4):
-            finish_direct(acc1[m], 1, m)
-        acc2 = [bank(4 + i) for i in range(4)]
-        multiply_direct(acc2, 2, PASS_ORDER)
-        gather_ts(2, "ts_direct")
-        for m in range(4):
-            finish_direct(acc2[m], 2, m)
-        acc3 = [bank(i) for i in range(4)]
-        multiply_direct(acc3, 3, PASS_ORDER)
-        gather_ts(3, "ts_direct")
-        for m in range(4):
-            finish_direct(acc3[m], 3, m, 2 if m == 3 else 1)
+        gather_words(C, 0, 1)
+        gather_words(C, 1, 2)
+        multiply(acc0, 0, (C,))
+        multiply(acc1, 1, (C,))
+        finish(acc0, 0)
+        gather_words(C, 2, 3, "picked0_0")
+        acc2 = [bank(i) for i in range(4)]
+        multiply(acc2, 2, PASS_ORDER)
+        finish(acc1, 1)
+        gather_words(C, 3, 4, "picked0_1")
+        acc3 = [bank(4 + i) for i in range(4)]
+        multiply(acc3, 3, PASS_ORDER)
+        finish(acc2, 2)
+        finish(acc3, 3)

@@ -15,6 +15,7 @@ U8 = mybir.dt.uint8
 FP8X4 = mybir.dt.float8_e4m3fn_x4
 FP4X4 = mybir.dt.float4_e2m1fn_x4
 GELU = mybir.ActivationFunctionType.Gelu_apprx_tanh
+COPY = mybir.ActivationFunctionType.Copy
 MULT = mybir.AluOpType.mult
 
 P = 128
@@ -29,6 +30,7 @@ def tile_list_tabts_gelu_kernel(tc, tab_words, tab_scales, w8, w4_words, w4_scal
     with ExitStack() as ctx:
         keep = ctx.enter_context(tc.tile_pool(name="keep", bufs=1))
         stage = ctx.enter_context(tc.tile_pool(name="stage", bufs=12))
+        pairs = ctx.enter_context(tc.tile_pool(name="pairs", bufs=8))
         psum = ctx.enter_context(tc.psum_pool(name="psum", bufs=1))
 
         def bank(i):
@@ -40,7 +42,7 @@ def tile_list_tabts_gelu_kernel(tc, tab_words, tab_scales, w8, w4_words, w4_scal
         scale_win = keep.tile([P, T // 4], I32, name="scale_win", align_bytes=64)
         nc.gpsimd.memset(scale_win[64:128, :], 0)
         nc.vector.memset(scale_win[32:64, :], 0)
-        nc.sync.dma_start(scale_win[0:32, :], tab_scales[1:3].rearrange("a q t -> (a q) t").bitcast(I32))
+        nc.sync.dma_start(scale_win[0:32, :], tab_scales[1:3].rearrange("a q t -> q a t").bitcast(I32))
         ts_rows = keep.tile([P, P], F32, name="ts_rows")
         nc.scalar.dma_start(ts_rows[0:32, :], ts[0].rearrange("(c p) -> c p", p=P))
         nc.sync.dma_start(scale_win[64:80, :], tab_scales[0].bitcast(I32))
@@ -93,27 +95,25 @@ def tile_list_tabts_gelu_kernel(tc, tab_words, tab_scales, w8, w4_words, w4_scal
         picked_scales = keep.tile([P, S // 4], I32, name="picked_scales", align_bytes=64)
         nc.vector.tensor_copy(picked_scales[:].bitcast(U8), scale_win[:].bitcast(U8).indirect(offsets[:]))
 
-        first_row = {1: 0, 2: 16, 0: 64}
-        plane_row = {1: 0, 2: 0, 0: 4}
-        plane_col = {1: 0, 2: 1, 0: 1}
+        low_words = slice(0, HALF // 4)
+        high_words = slice(HALF // 4, S // 4)
+        early = [(planes[0][r:P:32, a - 1, :], picked_scales[2 * r + a - 1 : 32 : 8, low_words]) for a in (1, 2) for r in range(4)]
+        early += [(planes[0][4 + r : P : 32, :, :].rearrange("p h w -> p (h w)"), picked_scales[64 + r : 80 : 4, :]) for r in range(4)]
+        late = [(planes[1][32 * q : 32 * q + 4, :, :], picked_scales[8 * q : 8 * q + 8, high_words]) for q in range(4)]
 
-        def move_scales(h, rows):
-            words = slice(h * HALF // 4, (h + 1) * HALF // 4)
-            for a, r in rows:
-                nc.sync.dma_start(
-                    planes[h][plane_row[a] + r : P : 32, plane_col[a], :],
-                    picked_scales[first_row[a] + r : first_row[a] + 16 : 4, words],
-                )
+        def move_scales(moves):
+            for plane_rows, picked_rows in moves:
+                nc.sync.dma_start(plane_rows, picked_rows)
 
-        rows = [(a, r) for a in PASS_ORDER for r in range(4)]
-        move_scales(0, rows[:6])
+        move_scales(early[:6])
         w8_raw = keep.tile([P, 4, M], F32, name="w8_raw")
         nc.sync.dma_start(w8_raw[:], w8.rearrange("(p j) n -> p j n", j=4))
-        move_scales(0, rows[6:])
+        move_scales(early[6:])
         load_table(C)
-        move_scales(1, rows)
+        move_scales(late)
 
         picked = {}
+        picked_ts = {}
         w8_codes = keep.tile([P, M], U32, name="w8_codes", align_bytes=64)
         w8_plane = keep.tile([P, M], U8, name="w8_plane", align_bytes=64)
 
@@ -124,60 +124,115 @@ def tile_list_tabts_gelu_kernel(tc, tab_words, tab_scales, w8, w4_words, w4_scal
             for s in range(s0, s1):
                 picked[a, s] = words[:, (s - s0) * NB : (s - s0 + 1) * NB]
 
-        def weights(a, m):
-            n0, n1 = m * P, (m + 1) * P
+        def weights(a, n0, n1):
             if a == 0:
                 return w8_codes[:, n0:n1].bitcast(FP8X4), w8_plane[:, n0:n1]
             return w4[:, a - 1, 2 * n0 : 2 * n1].bitcast(FP4X4), w4_plane[:, a - 1, :].bitcast(U8)[:, n0:n1]
 
+        def columns(a, s, j0, j1):
+            codes = picked[a, s][:, j0:j1].bitcast(FP8X4)
+            if a == 0:
+                return codes, planes[0][4:P, s // 2, :].bitcast(U8)[:, (s % 2) * NB + j0 : (s % 2) * NB + j1]
+            return codes, planes[s // 2][:, a - 1, :].bitcast(U8)[:, (s % 2) * NB + j0 : (s % 2) * NB + j1]
+
+        def mm(acc, a, lhs, rhs):
+            nc.tensor.matmul_mx(
+                out=acc[:], lhsT=lhs[0], lhsT_scale=lhs[1], rhs=rhs[0], rhs_scale=rhs[1],
+                start=(a == A), stop=(a == C),
+            )
+
         def multiply(accs, s, passes):
             for m in range(4):
                 for a in passes:
-                    codes, scales = weights(a, m)
-                    plane = planes[s // 2][plane_row[a] : P, plane_col[a], :].bitcast(U8)
-                    nc.tensor.matmul_mx(
-                        out=accs[m][:], lhsT=codes, lhsT_scale=scales,
-                        rhs=picked[a, s].bitcast(FP8X4), rhs_scale=plane[:, (s % 2) * NB : (s % 2 + 1) * NB],
-                        start=(a == A), stop=(a == C),
-                    )
+                    mm(accs[m], a, weights(a, m * P, (m + 1) * P), columns(a, s, 0, NB))
 
-        def finish(accs, s):
+        def multiply_turned(accs, s, a):
+            for i in range(4):
+                mm(accs[i], a, columns(a, s, i * P, (i + 1) * P), weights(a, 0, M))
+
+        def gather_ts(s0, s1, slot=None):
+            name = "picked_ts%d" % s0
+            values = keep.tile([P, (s1 - s0) * NB], F32, name=name, tag=slot or name, align_bytes=64)
+            nc.vector.tensor_copy(values[:], ts_win[:].indirect(offsets[:, s0 * 32 : s1 * 32]))
+            for s in range(s0, s1):
+                picked_ts[s] = values[:, (s - s0) * NB : (s - s0 + 1) * NB]
+
+        def turn_ts(s, free_bank):
+            part = keep.tile([P, 4], F32, name="ts_part%d" % s)
+            turned = bank(free_bank)
+            for i in range(4):
+                nc.tensor.transpose(turned[:, i * P : (i + 1) * P], picked_ts[s][:, i * P : (i + 1) * P], ident[:])
+            nc.scalar.copy(part[:], turned[:, 0:NB:P])
+            return part
+
+        def scale_turned(accs, s, part):
+            yt = keep.tile([P, 4, M], F32, name="yt%d" % s, align_bytes=64)
+            for i in range(4):
+                nc.scalar.activation(yt[:, i, :], accs[i][:], COPY, scale=part[:, i : i + 1])
+            return yt
+
+        def direct(acc, s, m, res, c0=0, c1=NB):
+            y = stage.tile([P, NB], F32, name="y")
+            nc.vector.tensor_tensor(y[:, c0:c1], acc[:, c0:c1], picked_ts[s][:, c0:c1], MULT)
+            nc.scalar.activation(res[:, s % 2, c0:c1], y[:, c0:c1], GELU, bias=bias[:, m : m + 1])
+
+        def turned_back(yt, s, m, res, free_bank):
+            back = bank(free_bank)
+            for i in range(4):
+                nc.tensor.transpose(back[:, i * P : (i + 1) * P], yt[:, i, m * P : (m + 1) * P], ident[:])
+            nc.scalar.activation(res[:, s % 2, :], back[:], GELU, bias=bias[:, m : m + 1])
+
+        def store(res, h, m, c0=0, c1=HALF):
+            nc.sync.dma_start(out[m * P : (m + 1) * P, h * HALF + c0 : h * HALF + c1], res[:].rearrange("p s j -> p (s j)")[:, c0:c1])
+
+        def multiply_tile(acc, s, m):
+            for a in PASS_ORDER:
+                mm(acc, a, weights(a, m * P, (m + 1) * P), columns(a, s, 0, NB))
+
+        def result():
+            return pairs.tile([P, 2, NB], F32, name="res")
+
+        def second_half(banks):
             for m in range(4):
-                y = stage.tile([P, NB], F32, name="y")
-                res = stage.tile([P, NB], F32, name="res")
-                width = NB // 2 if (s, m) == (3, 3) else NB
-                for c0 in range(0, NB, width):
-                    cols = slice(c0, c0 + width)
-                    tokens = slice(s * NB + c0, s * NB + c0 + width)
-                    nc.vector.tensor_tensor(y[:, cols], accs[m][:, cols], picked_ts[:, tokens], MULT)
-                    nc.scalar.activation(res[:, cols], y[:, cols], GELU, bias=bias[:, m : m + 1])
-                    nc.sync.dma_start(out[m * P : (m + 1) * P, tokens], res[:, cols])
+                accs = [bank(i) for i in banks[m]]
+                multiply_tile(accs[0], 2, m)
+                multiply_tile(accs[1], 3, m)
+                res = result()
+                direct(accs[0], 2, m, res)
+                if m < 3:
+                    direct(accs[1], 3, m, res)
+                    store(res, 1, m)
+                else:
+                    store(res, 1, m, 0, NB)
+                    for c0 in (0, NB // 2):
+                        direct(accs[1], 3, m, res, c0, c0 + NB // 2)
+                        store(res, 1, m, NB + c0, NB + c0 + NB // 2)
 
         gather_words(A, 0, 4)
-        picked_ts = keep.tile([P, S], F32, name="picked_ts", align_bytes=64)
-        nc.vector.tensor_copy(picked_ts[:], ts_win[:].indirect(offsets[:]))
+        gather_ts(0, 2)
+        part = turn_ts(0, 7)
         acc0 = [bank(i) for i in range(4)]
         acc1 = [bank(4 + i) for i in range(4)]
-        multiply(acc0, 0, (A,))
+        multiply_turned(acc0, 0, A)
         multiply(acc1, 1, (A,))
-        gather_words(B, 0, 2)
         gather_words(B, 2, 4)
-        multiply(acc0, 0, (B,))
+        gather_words(B, 0, 2)
+        multiply_turned(acc0, 0, B)
         multiply(acc1, 1, (B,))
         w8_grouped = keep.tile([P, M, 4], BF16, name="w8_grouped", align_bytes=64)
         nc.scalar.copy(w8_grouped[:], w8_raw[:].rearrange("p j n -> p n j"))
         nc.vector.quantize_mx(out=w8_codes[:].bitcast(FP8X4), scales=w8_plane[:], in_=w8_grouped[:].rearrange("p n j -> p (n j)"))
         gather_words(C, 0, 1)
         gather_words(C, 1, 2)
-        multiply(acc0, 0, (C,))
+        multiply_turned(acc0, 0, C)
         multiply(acc1, 1, (C,))
-        finish(acc0, 0)
+        yt = scale_turned(acc0, 0, part)
+        for m in range(4):
+            res = result()
+            direct(acc1[m], 1, m, res)
+            turned_back(yt, 0, m, res, m)
+            store(res, 0, m)
         gather_words(C, 2, 3, "picked0_0")
-        acc2 = [bank(i) for i in range(4)]
-        multiply(acc2, 2, PASS_ORDER)
-        finish(acc1, 1)
         gather_words(C, 3, 4, "picked0_1")
-        acc3 = [bank(4 + i) for i in range(4)]
-        multiply(acc3, 3, PASS_ORDER)
-        finish(acc2, 2)
-        finish(acc3, 3)
+        gather_ts(2, 4, "picked_ts0")
+        second_half([(4 + m, m) for m in range(4)])

@@ -19,22 +19,22 @@ COPY = mybir.ActivationFunctionType.Copy
 MULT = mybir.AluOpType.mult
 
 P = 128
-NB = 512
+SLICE = 512
+SLICE_COLS = SLICE // 16
 HALF = S // 2
-PASS_ORDER = (1, 2, 0)
+ROW_TILES = M // P
+FIRST, SECOND, LAST = 2, 1, 0
+MOVES_AHEAD_OF_W8 = 6
 
 
 def tile_list_tabts_gelu_kernel(tc, tab_words, tab_scales, w8, w4_words, w4_scales, ts, b, offs, out):
     nc = tc.nc
-    A, B, C = PASS_ORDER
     with ExitStack() as ctx:
         keep = ctx.enter_context(tc.tile_pool(name="keep", bufs=1))
-        stage = ctx.enter_context(tc.tile_pool(name="stage", bufs=12))
-        pairs = ctx.enter_context(tc.tile_pool(name="pairs", bufs=8))
         psum = ctx.enter_context(tc.psum_pool(name="psum", bufs=1))
 
         def bank(i):
-            return psum.tile([P, NB], F32, name="bank%d" % i, tag="bank%d" % i)
+            return psum.tile([P, SLICE], F32, name="bank%d" % i, tag="bank%d" % i)
 
         offsets = keep.tile([P, S // 16], U16, name="offsets")
         nc.sync.dma_start(offsets[:], offs)
@@ -42,7 +42,7 @@ def tile_list_tabts_gelu_kernel(tc, tab_words, tab_scales, w8, w4_words, w4_scal
         scale_win = keep.tile([P, T // 4], I32, name="scale_win", align_bytes=64)
         nc.gpsimd.memset(scale_win[64:128, :], 0)
         nc.vector.memset(scale_win[32:64, :], 0)
-        nc.sync.dma_start(scale_win[0:32, :], tab_scales[1:3].rearrange("a q t -> q a t").bitcast(I32))
+        nc.sync.dma_start(scale_win[0:32, :], tab_scales[1:3].rearrange("a n t -> n a t").bitcast(I32))
         ts_rows = keep.tile([P, P], F32, name="ts_rows")
         nc.scalar.dma_start(ts_rows[0:32, :], ts[0].rearrange("(c p) -> c p", p=P))
         nc.sync.dma_start(scale_win[64:80, :], tab_scales[0].bitcast(I32))
@@ -51,65 +51,72 @@ def tile_list_tabts_gelu_kernel(tc, tab_words, tab_scales, w8, w4_words, w4_scal
         b_rows = keep.tile([P, P], F32, name="b_rows")
         nc.vector.memset(b_rows[:], 0.0)
 
-        table = {a: keep.tile([P, T], I32, name="table%d" % a, align_bytes=64) for a in PASS_ORDER}
+        table = {a: keep.tile([P, T], I32, name="table%d" % a, align_bytes=64) for a in (FIRST, SECOND, LAST)}
 
         def load_table(a):
             nc.sync.dma_start(table[a][:], tab_words[a].rearrange("p t i -> p (t i)").bitcast(I32))
 
-        load_table(A)
+        load_table(FIRST)
         w4 = keep.tile([P, 2, 2 * M], U8, name="w4", align_bytes=64)
         nc.sync.dma_start(w4[:].bitcast(I32), w4_words.rearrange("a p n -> p a n").bitcast(I32))
         w4_plane = keep.tile([P, 2, M // 4], I32, name="w4_plane", align_bytes=64)
         nc.vector.memset(w4_plane[:], 0)
         for r in range(4):
             nc.sync.dma_start(w4_plane[r:P:32, :, :], w4_scales[:, r:16:4, :].rearrange("a q n -> q a n").bitcast(I32))
-        nc.sync.dma_start(b_rows[0:4, :], b.rearrange("(m p) -> m p", p=P))
-        load_table(B)
+        nc.sync.dma_start(b_rows[0:ROW_TILES, :], b.rearrange("(m p) -> m p", p=P))
+        load_table(SECOND)
 
         warm = keep.tile([P, 2], F32, name="warm")
         nc.vector.memset(warm[:, 0:1], 0.0)
         nc.scalar.activation(warm[:, 1:2], warm[:, 0:1], GELU)
-        planes = [keep.tile([P, 2, HALF // 4], I32, name="planes%d" % h, align_bytes=64) for h in range(2)]
-        for h in range(2):
-            nc.vector.memset(planes[h][:], 0)
+
+        planes = keep.tile([P, 4, HALF // 4], I32, name="planes", align_bytes=64)
+        nc.vector.memset(planes[:], 0)
+        block = {(2, 0): 0, (1, 0): 1, (1, 1): 2, (2, 1): 3, (0, 0): 1, (0, 1): 2}
 
         ident = keep.tile([P, P], F32, name="ident")
         make_identity(nc, ident[:])
-
-        ts_cols = keep.tile([P, 32], F32, name="ts_cols")
-        first = bank(0)
-        nc.tensor.transpose(first[:, 0:P], ts_rows[:], ident[:])
-        nc.scalar.copy(ts_cols[:], first[:, 0:32])
+        ts_cols = keep.tile([P, T // P], F32, name="ts_cols")
+        ts_turned = bank(0)
+        nc.tensor.transpose(ts_turned[:, 0:P], ts_rows[:], ident[:])
+        nc.scalar.copy(ts_cols[:], ts_turned[:, 0 : T // P])
         ts_win = keep.tile([P, T], F32, name="ts_win", align_bytes=64)
-        for g in range(T // NB):
+        for g in range(T // SLICE):
             spread = bank(1 + g % 4)
             for c in range(4):
                 col = 4 * g + c
                 nc.tensor.transpose(spread[:, c * P : (c + 1) * P], ts_cols[:, col : col + 1].to_broadcast([P, P]), ident[:])
-            nc.scalar.copy(ts_win[:, g * NB : (g + 1) * NB], spread[:])
-        bias = keep.tile([P, 4], F32, name="bias")
+            nc.scalar.copy(ts_win[:, g * SLICE : (g + 1) * SLICE], spread[:])
+        bias = keep.tile([P, ROW_TILES], F32, name="bias")
         b_turned = bank(5)
         nc.tensor.transpose(b_turned[:, 0:P], b_rows[:], ident[:])
-        nc.scalar.copy(bias[:], b_turned[:, 0:4])
+        nc.scalar.copy(bias[:], b_turned[:, 0:ROW_TILES])
 
         picked_scales = keep.tile([P, S // 4], I32, name="picked_scales", align_bytes=64)
         nc.vector.tensor_copy(picked_scales[:].bitcast(U8), scale_win[:].bitcast(U8).indirect(offsets[:]))
 
         low_words = slice(0, HALF // 4)
         high_words = slice(HALF // 4, S // 4)
-        early = [(planes[0][r:P:32, a - 1, :], picked_scales[2 * r + a - 1 : 32 : 8, low_words]) for a in (1, 2) for r in range(4)]
-        early += [(planes[0][4 + r : P : 32, :, :].rearrange("p h w -> p (h w)"), picked_scales[64 + r : 80 : 4, :]) for r in range(4)]
-        late = [(planes[1][32 * q : 32 * q + 4, :, :], picked_scales[8 * q : 8 * q + 8, high_words]) for q in range(4)]
+        early = [
+            (planes[r:P:32, block[a, 0], :], picked_scales[2 * r + a - 1 : 32 : 8, low_words])
+            for a in (FIRST, SECOND)
+            for r in range(4)
+        ]
+        early += [
+            (planes[4 + r : P : 32, 1:3, :].rearrange("p h w -> p (h w)"), picked_scales[64 + r : 80 : 4, :])
+            for r in range(4)
+        ]
+        late = [(planes[32 * q : 32 * q + 4, 2:4, :], picked_scales[8 * q : 8 * q + 8, high_words]) for q in range(4)]
 
         def move_scales(moves):
             for plane_rows, picked_rows in moves:
                 nc.sync.dma_start(plane_rows, picked_rows)
 
-        move_scales(early[:6])
+        move_scales(early[:MOVES_AHEAD_OF_W8])
         w8_raw = keep.tile([P, 4, M], F32, name="w8_raw")
-        nc.sync.dma_start(w8_raw[:], w8.rearrange("(p j) n -> p j n", j=4))
-        move_scales(early[6:])
-        load_table(C)
+        nc.sync.dma_start(w8_raw[:], w8.rearrange("(p i) n -> p i n", i=4))
+        move_scales(early[MOVES_AHEAD_OF_W8:])
+        load_table(LAST)
         move_scales(late)
 
         picked = {}
@@ -117,12 +124,22 @@ def tile_list_tabts_gelu_kernel(tc, tab_words, tab_scales, w8, w4_words, w4_scal
         w8_codes = keep.tile([P, M], U32, name="w8_codes", align_bytes=64)
         w8_plane = keep.tile([P, M], U8, name="w8_plane", align_bytes=64)
 
-        def gather_words(a, s0, s1, slot=None):
+        def entries(s0, s1):
+            return offsets[:, s0 * SLICE_COLS : s1 * SLICE_COLS]
+
+        def gather_words(a, s0, s1, reuse=None):
             name = "picked%d_%d" % (a, s0)
-            words = keep.tile([P, (s1 - s0) * NB], U32, name=name, tag=slot or name, align_bytes=64)
-            nc.vector.tensor_copy(words[:], table[a][:].bitcast(U32).indirect(offsets[:, s0 * 32 : s1 * 32]))
+            words = keep.tile([P, (s1 - s0) * SLICE], U32, name=name, tag=reuse or name, align_bytes=64)
+            nc.vector.tensor_copy(words[:], table[a][:].bitcast(U32).indirect(entries(s0, s1)))
             for s in range(s0, s1):
-                picked[a, s] = words[:, (s - s0) * NB : (s - s0 + 1) * NB]
+                picked[a, s] = words[:, (s - s0) * SLICE : (s - s0 + 1) * SLICE]
+
+        def gather_ts(s0, s1, reuse=None):
+            name = "picked_ts%d" % s0
+            values = keep.tile([P, (s1 - s0) * SLICE], F32, name=name, tag=reuse or name, align_bytes=64)
+            nc.vector.tensor_copy(values[:], ts_win[:].indirect(entries(s0, s1)))
+            for s in range(s0, s1):
+                picked_ts[s] = values[:, (s - s0) * SLICE : (s - s0 + 1) * SLICE]
 
         def weights(a, n0, n1):
             if a == 0:
@@ -130,109 +147,82 @@ def tile_list_tabts_gelu_kernel(tc, tab_words, tab_scales, w8, w4_words, w4_scal
             return w4[:, a - 1, 2 * n0 : 2 * n1].bitcast(FP4X4), w4_plane[:, a - 1, :].bitcast(U8)[:, n0:n1]
 
         def columns(a, s, j0, j1):
-            codes = picked[a, s][:, j0:j1].bitcast(FP8X4)
-            if a == 0:
-                return codes, planes[0][4:P, s // 2, :].bitcast(U8)[:, (s % 2) * NB + j0 : (s % 2) * NB + j1]
-            return codes, planes[s // 2][:, a - 1, :].bitcast(U8)[:, (s % 2) * NB + j0 : (s % 2) * NB + j1]
+            plane = planes[4 if a == 0 else 0 : P, block[a, s // 2], :].bitcast(U8)
+            start = (s % 2) * SLICE
+            return picked[a, s][:, j0:j1].bitcast(FP8X4), plane[:, start + j0 : start + j1]
 
-        def mm(acc, a, lhs, rhs):
+        def add_pass(acc, a, stationary, moving):
             nc.tensor.matmul_mx(
-                out=acc[:], lhsT=lhs[0], lhsT_scale=lhs[1], rhs=rhs[0], rhs_scale=rhs[1],
-                start=(a == A), stop=(a == C),
+                out=acc[:],
+                lhsT=stationary[0],
+                lhsT_scale=stationary[1],
+                rhs=moving[0],
+                rhs_scale=moving[1],
+                start=(a == FIRST),
+                stop=(a == LAST),
             )
 
-        def multiply(accs, s, passes):
-            for m in range(4):
-                for a in passes:
-                    mm(accs[m], a, weights(a, m * P, (m + 1) * P), columns(a, s, 0, NB))
+        def add_pass_direct(acc, a, s, m):
+            add_pass(acc, a, weights(a, m * P, (m + 1) * P), columns(a, s, 0, SLICE))
 
-        def multiply_turned(accs, s, a):
-            for i in range(4):
-                mm(accs[i], a, columns(a, s, i * P, (i + 1) * P), weights(a, 0, M))
+        def add_pass_low_half(a):
+            for i in range(SLICE // P):
+                add_pass(turned_sums[i], a, columns(a, 0, i * P, (i + 1) * P), weights(a, 0, M))
+            for m in range(ROW_TILES):
+                add_pass_direct(slice1_sums[m], a, 1, m)
 
-        def gather_ts(s0, s1, slot=None):
-            name = "picked_ts%d" % s0
-            values = keep.tile([P, (s1 - s0) * NB], F32, name=name, tag=slot or name, align_bytes=64)
-            nc.vector.tensor_copy(values[:], ts_win[:].indirect(offsets[:, s0 * 32 : s1 * 32]))
-            for s in range(s0, s1):
-                picked_ts[s] = values[:, (s - s0) * NB : (s - s0 + 1) * NB]
-
-        def turn_ts(s, free_bank):
-            part = keep.tile([P, 4], F32, name="ts_part%d" % s)
-            turned = bank(free_bank)
-            for i in range(4):
-                nc.tensor.transpose(turned[:, i * P : (i + 1) * P], picked_ts[s][:, i * P : (i + 1) * P], ident[:])
-            nc.scalar.copy(part[:], turned[:, 0:NB:P])
-            return part
-
-        def scale_turned(accs, s, part):
-            yt = keep.tile([P, 4, M], F32, name="yt%d" % s, align_bytes=64)
-            for i in range(4):
-                nc.scalar.activation(yt[:, i, :], accs[i][:], COPY, scale=part[:, i : i + 1])
-            return yt
-
-        def direct(acc, s, m, res, c0=0, c1=NB):
-            y = stage.tile([P, NB], F32, name="y")
+        def finish_direct(acc, s, m, res, c0, c1):
+            y = keep.tile([P, SLICE], F32, name="y%d_%d_%d" % (s, m, c0), align_bytes=64)
             nc.vector.tensor_tensor(y[:, c0:c1], acc[:, c0:c1], picked_ts[s][:, c0:c1], MULT)
-            nc.scalar.activation(res[:, s % 2, c0:c1], y[:, c0:c1], GELU, bias=bias[:, m : m + 1])
+            nc.scalar.activation(res[:, c0:c1], y[:, c0:c1], GELU, bias=bias[:, m : m + 1])
 
-        def turned_back(yt, s, m, res, free_bank):
-            back = bank(free_bank)
-            for i in range(4):
-                nc.tensor.transpose(back[:, i * P : (i + 1) * P], yt[:, i, m * P : (m + 1) * P], ident[:])
-            nc.scalar.activation(res[:, s % 2, :], back[:], GELU, bias=bias[:, m : m + 1])
-
-        def store(res, h, m, c0=0, c1=HALF):
-            nc.sync.dma_start(out[m * P : (m + 1) * P, h * HALF + c0 : h * HALF + c1], res[:].rearrange("p s j -> p (s j)")[:, c0:c1])
-
-        def multiply_tile(acc, s, m):
-            for a in PASS_ORDER:
-                mm(acc, a, weights(a, m * P, (m + 1) * P), columns(a, s, 0, NB))
-
-        def result():
-            return pairs.tile([P, 2, NB], F32, name="res")
-
-        def second_half(banks):
-            for m in range(4):
-                accs = [bank(i) for i in banks[m]]
-                multiply_tile(accs[0], 2, m)
-                multiply_tile(accs[1], 3, m)
-                res = result()
-                direct(accs[0], 2, m, res)
-                if m < 3:
-                    direct(accs[1], 3, m, res)
-                    store(res, 1, m)
-                else:
-                    store(res, 1, m, 0, NB)
-                    for c0 in (0, NB // 2):
-                        direct(accs[1], 3, m, res, c0, c0 + NB // 2)
-                        store(res, 1, m, NB + c0, NB + c0 + NB // 2)
-
-        gather_words(A, 0, 4)
+        gather_words(FIRST, 0, 4)
         gather_ts(0, 2)
-        part = turn_ts(0, 7)
-        acc0 = [bank(i) for i in range(4)]
-        acc1 = [bank(4 + i) for i in range(4)]
-        multiply_turned(acc0, 0, A)
-        multiply(acc1, 1, (A,))
-        gather_words(B, 2, 4)
-        gather_words(B, 0, 2)
-        multiply_turned(acc0, 0, B)
-        multiply(acc1, 1, (B,))
+        ts_part = keep.tile([P, SLICE // P], F32, name="ts_part")
+        picked_turned = bank(7)
+        for i in range(SLICE // P):
+            nc.tensor.transpose(picked_turned[:, i * P : (i + 1) * P], picked_ts[0][:, i * P : (i + 1) * P], ident[:])
+        nc.scalar.copy(ts_part[:], picked_turned[:, 0:SLICE:P])
+        turned_sums = [bank(i) for i in range(SLICE // P)]
+        slice1_sums = [bank(4 + m) for m in range(ROW_TILES)]
+        add_pass_low_half(FIRST)
+        gather_words(SECOND, 0, 2)
+        gather_words(SECOND, 2, 4)
+        add_pass_low_half(SECOND)
         w8_grouped = keep.tile([P, M, 4], BF16, name="w8_grouped", align_bytes=64)
-        nc.scalar.copy(w8_grouped[:], w8_raw[:].rearrange("p j n -> p n j"))
-        nc.vector.quantize_mx(out=w8_codes[:].bitcast(FP8X4), scales=w8_plane[:], in_=w8_grouped[:].rearrange("p n j -> p (n j)"))
-        gather_words(C, 0, 1)
-        gather_words(C, 1, 2)
-        multiply_turned(acc0, 0, C)
-        multiply(acc1, 1, (C,))
-        yt = scale_turned(acc0, 0, part)
-        for m in range(4):
-            res = result()
-            direct(acc1[m], 1, m, res)
-            turned_back(yt, 0, m, res, m)
-            store(res, 0, m)
-        gather_words(C, 2, 3, "picked0_0")
-        gather_words(C, 3, 4, "picked0_1")
-        gather_ts(2, 4, "picked_ts0")
-        second_half([(4 + m, m) for m in range(4)])
+        nc.scalar.copy(w8_grouped[:], w8_raw[:].rearrange("p i n -> p n i"))
+        nc.vector.quantize_mx(out=w8_codes[:].bitcast(FP8X4), scales=w8_plane[:], in_=w8_grouped[:].rearrange("p n i -> p (n i)"))
+
+        gather_words(LAST, 0, 1)
+        gather_words(LAST, 1, 2)
+        add_pass_low_half(LAST)
+        scaled = keep.tile([P, SLICE // P, M], F32, name="scaled", align_bytes=64)
+        for i in range(SLICE // P):
+            nc.scalar.activation(scaled[:, i, :], turned_sums[i][:], COPY, scale=ts_part[:, i : i + 1])
+        for m in range(ROW_TILES):
+            pair = keep.tile([P, HALF], F32, name="pair%d" % m)
+            finish_direct(slice1_sums[m], 1, m, pair[:, SLICE:HALF], 0, SLICE)
+            back = bank(m)
+            for i in range(SLICE // P):
+                nc.tensor.transpose(back[:, i * P : (i + 1) * P], scaled[:, i, m * P : (m + 1) * P], ident[:])
+            nc.scalar.activation(pair[:, 0:SLICE], back[:], GELU, bias=bias[:, m : m + 1])
+            nc.sync.dma_start(out[m * P : (m + 1) * P, 0:HALF], pair[:])
+
+        gather_words(LAST, 2, 3, reuse="picked0_0")
+        gather_ts(2, 3, reuse="picked0_1")
+        gather_words(LAST, 3, 4, reuse="picked_ts0")
+
+        def direct_slice(s, first_bank, last_pieces):
+            for m in range(ROW_TILES):
+                acc = bank(first_bank + m)
+                for a in (FIRST, SECOND, LAST):
+                    add_pass_direct(acc, a, s, m)
+                res = keep.tile([P, SLICE], F32, name="res%d_%d" % (s, m))
+                width = SLICE // last_pieces if m == ROW_TILES - 1 else SLICE
+                for c0 in range(0, SLICE, width):
+                    finish_direct(acc, s, m, res, c0, c0 + width)
+                    nc.sync.dma_start(out[m * P : (m + 1) * P, s * SLICE + c0 : s * SLICE + c0 + width], res[:, c0 : c0 + width])
+
+        direct_slice(2, 4, 1)
+        gather_ts(3, 4, reuse="y1_3_0")
+        direct_slice(3, 0, 2)

@@ -25,6 +25,7 @@ HALF = S // 2
 ROW_TILES = M // P
 FIRST, SECOND, LAST = 2, 1, 0
 MOVES_AHEAD_OF_W8 = 6
+STORED_APART = 2
 
 
 def tile_list_tabts_gelu_kernel(tc, tab_words, tab_scales, w8, w4_words, w4_scales, ts, b, offs, out):
@@ -65,10 +66,6 @@ def tile_list_tabts_gelu_kernel(tc, tab_words, tab_scales, w8, w4_words, w4_scal
             nc.sync.dma_start(w4_plane[r:P:32, :, :], w4_scales[:, r:16:4, :].rearrange("a q n -> q a n").bitcast(I32))
         nc.sync.dma_start(b_rows[0:ROW_TILES, :], b.rearrange("(m p) -> m p", p=P))
         load_table(SECOND)
-
-        warm = keep.tile([P, 2], F32, name="warm")
-        nc.vector.memset(warm[:, 0:1], 0.0)
-        nc.scalar.activation(warm[:, 1:2], warm[:, 0:1], GELU)
 
         planes = keep.tile([P, 4, HALF // 4], I32, name="planes", align_bytes=64)
         nc.vector.memset(planes[:], 0)
@@ -165,11 +162,16 @@ def tile_list_tabts_gelu_kernel(tc, tab_words, tab_scales, w8, w4_words, w4_scal
         def add_pass_direct(acc, a, s, m):
             add_pass(acc, a, weights(a, m * P, (m + 1) * P), columns(a, s, 0, SLICE))
 
-        def add_pass_low_half(a):
+        def add_pass_slice0(a):
             for i in range(SLICE // P):
                 add_pass(turned_sums[i], a, columns(a, 0, i * P, (i + 1) * P), weights(a, 0, M))
+
+        def add_pass_slice1(a):
             for m in range(ROW_TILES):
                 add_pass_direct(slice1_sums[m], a, 1, m)
+
+        def store(res, m, j0, j1):
+            nc.sync.dma_start(out[m * P : (m + 1) * P, j0:j1], res)
 
         def finish_direct(acc, s, m, res, c0, c1):
             y = keep.tile([P, SLICE], F32, name="y%d_%d_%d" % (s, m, c0), align_bytes=64)
@@ -185,31 +187,43 @@ def tile_list_tabts_gelu_kernel(tc, tab_words, tab_scales, w8, w4_words, w4_scal
         nc.scalar.copy(ts_part[:], picked_turned[:, 0:SLICE:P])
         turned_sums = [bank(i) for i in range(SLICE // P)]
         slice1_sums = [bank(4 + m) for m in range(ROW_TILES)]
-        add_pass_low_half(FIRST)
+        add_pass_slice0(FIRST)
+        add_pass_slice1(FIRST)
         gather_words(SECOND, 0, 2)
         gather_words(SECOND, 2, 4)
-        add_pass_low_half(SECOND)
+        add_pass_slice0(SECOND)
+        add_pass_slice1(SECOND)
         w8_grouped = keep.tile([P, M, 4], BF16, name="w8_grouped", align_bytes=64)
         nc.scalar.copy(w8_grouped[:], w8_raw[:].rearrange("p i n -> p n i"))
         nc.vector.quantize_mx(out=w8_codes[:].bitcast(FP8X4), scales=w8_plane[:], in_=w8_grouped[:].rearrange("p n i -> p (n i)"))
 
-        gather_words(LAST, 0, 1)
         gather_words(LAST, 1, 2)
-        add_pass_low_half(LAST)
+        gather_words(LAST, 0, 1)
+        add_pass_slice1(LAST)
+        add_pass_slice0(LAST)
+        pairs = [keep.tile([P, HALF], F32, name="pair%d" % m) for m in range(ROW_TILES)]
+
+        def finish_slice1(m):
+            finish_direct(slice1_sums[m], 1, m, pairs[m][:, SLICE:HALF], 0, SLICE)
+            if m < STORED_APART:
+                store(pairs[m][:, SLICE:HALF], m, SLICE, HALF)
+
+        finish_slice1(0)
         scaled = keep.tile([P, SLICE // P, M], F32, name="scaled", align_bytes=64)
         for i in range(SLICE // P):
             nc.scalar.activation(scaled[:, i, :], turned_sums[i][:], COPY, scale=ts_part[:, i : i + 1])
         for m in range(ROW_TILES):
-            pair = keep.tile([P, HALF], F32, name="pair%d" % m)
-            finish_direct(slice1_sums[m], 1, m, pair[:, SLICE:HALF], 0, SLICE)
+            if m > 0:
+                finish_slice1(m)
             back = bank(m)
             for i in range(SLICE // P):
                 nc.tensor.transpose(back[:, i * P : (i + 1) * P], scaled[:, i, m * P : (m + 1) * P], ident[:])
-            nc.scalar.activation(pair[:, 0:SLICE], back[:], GELU, bias=bias[:, m : m + 1])
-            nc.sync.dma_start(out[m * P : (m + 1) * P, 0:HALF], pair[:])
+            nc.scalar.activation(pairs[m][:, 0:SLICE], back[:], GELU, bias=bias[:, m : m + 1])
+            width = SLICE if m < STORED_APART else HALF
+            store(pairs[m][:, 0:width], m, 0, width)
 
-        gather_words(LAST, 2, 3, reuse="picked0_0")
-        gather_ts(2, 3, reuse="picked0_1")
+        gather_words(LAST, 2, 3, reuse="picked0_1")
+        gather_ts(2, 3, reuse="picked0_0")
         gather_words(LAST, 3, 4, reuse="picked_ts0")
 
         def direct_slice(s, first_bank, last_pieces):
@@ -221,7 +235,7 @@ def tile_list_tabts_gelu_kernel(tc, tab_words, tab_scales, w8, w4_words, w4_scal
                 width = SLICE // last_pieces if m == ROW_TILES - 1 else SLICE
                 for c0 in range(0, SLICE, width):
                     finish_direct(acc, s, m, res, c0, c0 + width)
-                    nc.sync.dma_start(out[m * P : (m + 1) * P, s * SLICE + c0 : s * SLICE + c0 + width], res[:, c0 : c0 + width])
+                    store(res[:, c0 : c0 + width], m, s * SLICE + c0, s * SLICE + c0 + width)
 
         direct_slice(2, 4, 1)
         gather_ts(3, 4, reuse="y1_3_0")

@@ -41,12 +41,12 @@ def tile_list_tabts_gelu_kernel(tc, tab_words, tab_scales, w8, w4_words, w4_scal
         nc.sync.dma_start(offsets[:], offs)
 
         scale_win = keep.tile([P, T // 4], I32, name="scale_win", align_bytes=64)
-        nc.gpsimd.memset(scale_win[64:128, :], 0)
+        nc.gpsimd.memset(scale_win[64:112, :], 0)
         nc.vector.memset(scale_win[32:64, :], 0)
         nc.sync.dma_start(scale_win[0:32, :], tab_scales[1:3].rearrange("a n t -> n a t").bitcast(I32))
         ts_rows = keep.tile([P, P], F32, name="ts_rows")
         nc.scalar.dma_start(ts_rows[0:32, :], ts[0].rearrange("(c p) -> c p", p=P))
-        nc.sync.dma_start(scale_win[64:80, :], tab_scales[0].bitcast(I32))
+        nc.sync.dma_start(scale_win[112:128, :], tab_scales[0].bitcast(I32))
         nc.vector.memset(ts_rows[32:64, :], 0.0)
         nc.vector.memset(ts_rows[64:128, :], 0.0)
         b_rows = keep.tile([P, P], F32, name="b_rows")
@@ -68,7 +68,7 @@ def tile_list_tabts_gelu_kernel(tc, tab_words, tab_scales, w8, w4_words, w4_scal
         load_table(SECOND)
 
         planes = keep.tile([P, 4, HALF // 4], I32, name="planes", align_bytes=64)
-        nc.vector.memset(planes[:], 0)
+        nc.gpsimd.memset(planes[:], 0)
         block = {(2, 0): 0, (1, 0): 1, (1, 1): 2, (2, 1): 3, (0, 0): 1, (0, 1): 2}
 
         ident = keep.tile([P, P], F32, name="ident")
@@ -100,7 +100,7 @@ def tile_list_tabts_gelu_kernel(tc, tab_words, tab_scales, w8, w4_words, w4_scal
             for r in range(4)
         ]
         early += [
-            (planes[4 + r : P : 32, 1:3, :].rearrange("p h w -> p (h w)"), picked_scales[64 + r : 80 : 4, :])
+            (planes[4 + r : P : 32, 1:3, :].rearrange("p h w -> p (h w)"), picked_scales[112 + r : 128 : 4, :])
             for r in range(4)
         ]
         late = [(planes[32 * q : 32 * q + 4, 2:4, :], picked_scales[8 * q : 8 * q + 8, high_words]) for q in range(4)]

@@ -45,8 +45,8 @@ def tile_list_tabts_gelu_kernel(tc, tab_words, tab_scales, w8, w4_words, w4_scal
         nc.vector.memset(scale_win[32:64, :], 0)
         nc.sync.dma_start(scale_win[0:32, :], tab_scales[1:3].rearrange("a n t -> n a t").bitcast(I32))
         ts_rows = keep.tile([P, P], F32, name="ts_rows")
-        nc.scalar.dma_start(ts_rows[0:32, :], ts[0].rearrange("(c p) -> c p", p=P))
-        nc.sync.dma_start(scale_win[112:128, :], tab_scales[0].bitcast(I32))
+        nc.sync.dma_start(ts_rows[0:32, :], ts[0].rearrange("(c p) -> c p", p=P))
+        nc.scalar.dma_start(scale_win[112:128, :], tab_scales[0].bitcast(I32))
         nc.vector.memset(ts_rows[32:64, :], 0.0)
         nc.vector.memset(ts_rows[64:128, :], 0.0)
         b_rows = keep.tile([P, P], F32, name="b_rows")
@@ -67,8 +67,6 @@ def tile_list_tabts_gelu_kernel(tc, tab_words, tab_scales, w8, w4_words, w4_scal
         nc.sync.dma_start(b_rows[0:ROW_TILES, :], b.rearrange("(m p) -> m p", p=P))
         load_table(SECOND)
 
-        planes = keep.tile([P, 4, HALF // 4], I32, name="planes", align_bytes=64)
-        nc.gpsimd.memset(planes[:], 0)
         block = {(2, 0): 0, (1, 0): 1, (1, 1): 2, (2, 1): 3, (0, 0): 1, (0, 1): 2}
 
         ident = keep.tile([P, P], F32, name="ident")
@@ -92,6 +90,7 @@ def tile_list_tabts_gelu_kernel(tc, tab_words, tab_scales, w8, w4_words, w4_scal
         picked_scales = keep.tile([P, S // 4], I32, name="picked_scales", align_bytes=64)
         nc.vector.tensor_copy(picked_scales[:].bitcast(U8), scale_win[:].bitcast(U8).indirect(offsets[:]))
 
+        planes = keep.tile([P, 4, HALF // 4], I32, name="planes", tag="scale_win", align_bytes=64)
         low_words = slice(0, HALF // 4)
         high_words = slice(HALF // 4, S // 4)
         early = [

@@ -38,12 +38,12 @@ def tile_list_tabts_gelu_kernel(tc, tab_words, tab_scales, w8, w4_words, w4_scal
             return psum.tile([P, SLICE], F32, name="bank%d" % i, tag="bank%d" % i)
 
         offsets = keep.tile([P, S // 16], U16, name="offsets")
-        nc.sync.dma_start(offsets[:], offs)
 
         scale_win = keep.tile([P, T // 4], I32, name="scale_win", align_bytes=64)
         nc.gpsimd.memset(scale_win[64:112, :], 0)
         nc.vector.memset(scale_win[32:64, :], 0)
         nc.sync.dma_start(scale_win[0:32, :], tab_scales[1:3].rearrange("a n t -> n a t").bitcast(I32))
+        nc.sync.dma_start(offsets[:], offs)
         ts_rows = keep.tile([P, P], F32, name="ts_rows")
         nc.sync.dma_start(ts_rows[0:32, :], ts[0].rearrange("(c p) -> c p", p=P))
         nc.scalar.dma_start(scale_win[112:128, :], tab_scales[0].bitcast(I32))
@@ -67,8 +67,6 @@ def tile_list_tabts_gelu_kernel(tc, tab_words, tab_scales, w8, w4_words, w4_scal
         nc.sync.dma_start(b_rows[0:ROW_TILES, :], b.rearrange("(m p) -> m p", p=P))
         load_table(SECOND)
 
-        block = {(2, 0): 0, (1, 0): 1, (1, 1): 2, (2, 1): 3, (0, 0): 1, (0, 1): 2}
-
         ident = keep.tile([P, P], F32, name="ident")
         make_identity(nc, ident[:])
         ts_cols = keep.tile([P, T // P], F32, name="ts_cols")
@@ -91,6 +89,7 @@ def tile_list_tabts_gelu_kernel(tc, tab_words, tab_scales, w8, w4_words, w4_scal
         nc.vector.tensor_copy(picked_scales[:].bitcast(U8), scale_win[:].bitcast(U8).indirect(offsets[:]))
 
         planes = keep.tile([P, 4, HALF // 4], I32, name="planes", tag="scale_win", align_bytes=64)
+        block = {(2, 0): 0, (1, 0): 1, (1, 1): 2, (2, 1): 3, (0, 0): 1, (0, 1): 2}
         low_words = slice(0, HALF // 4)
         high_words = slice(HALF // 4, S // 4)
         early = [

@@ -25,7 +25,7 @@ HALF = S // 2
 ROW_TILES = M // P
 FIRST, SECOND, LAST = 2, 1, 0
 MOVES_AHEAD_OF_W8 = 6
-STORED_APART = 2
+STORED_APART = 1
 
 
 def tile_list_tabts_gelu_kernel(tc, tab_words, tab_scales, w8, w4_words, w4_scales, ts, b, offs, out):
@@ -51,6 +51,9 @@ def tile_list_tabts_gelu_kernel(tc, tab_words, tab_scales, w8, w4_words, w4_scal
         nc.vector.memset(ts_rows[64:128, :], 0.0)
         b_rows = keep.tile([P, P], F32, name="b_rows")
         nc.vector.memset(b_rows[:], 0.0)
+
+        warm = keep.tile([P, 1], F32, name="warm")
+        nc.scalar.activation(warm[64:128, :], ts_rows[64:128, 0:1], GELU)
 
         table = {a: keep.tile([P, T], I32, name="table%d" % a, align_bytes=64) for a in (FIRST, SECOND, LAST)}
 
@@ -195,10 +198,10 @@ def tile_list_tabts_gelu_kernel(tc, tab_words, tab_scales, w8, w4_words, w4_scal
         nc.scalar.copy(w8_grouped[:], w8_raw[:].rearrange("p i n -> p n i"))
         nc.vector.quantize_mx(out=w8_codes[:].bitcast(FP8X4), scales=w8_plane[:], in_=w8_grouped[:].rearrange("p n i -> p (n i)"))
 
-        gather_words(LAST, 1, 2)
         gather_words(LAST, 0, 1)
-        add_pass_slice1(LAST)
+        gather_words(LAST, 1, 2)
         add_pass_slice0(LAST)
+        add_pass_slice1(LAST)
         pairs = [keep.tile([P, HALF], F32, name="pair%d" % m) for m in range(ROW_TILES)]
 
         def finish_slice1(m):
@@ -206,13 +209,11 @@ def tile_list_tabts_gelu_kernel(tc, tab_words, tab_scales, w8, w4_words, w4_scal
             if m < STORED_APART:
                 store(pairs[m][:, SLICE:HALF], m, SLICE, HALF)
 
-        finish_slice1(0)
         scaled = keep.tile([P, SLICE // P, M], F32, name="scaled", align_bytes=64)
         for i in range(SLICE // P):
             nc.scalar.activation(scaled[:, i, :], turned_sums[i][:], COPY, scale=ts_part[:, i : i + 1])
         for m in range(ROW_TILES):
-            if m > 0:
-                finish_slice1(m)
+            finish_slice1(m)
             back = bank(m)
             for i in range(SLICE // P):
                 nc.tensor.transpose(back[:, i * P : (i + 1) * P], scaled[:, i, m * P : (m + 1) * P], ident[:])
@@ -220,8 +221,8 @@ def tile_list_tabts_gelu_kernel(tc, tab_words, tab_scales, w8, w4_words, w4_scal
             width = SLICE if m < STORED_APART else HALF
             store(pairs[m][:, 0:width], m, 0, width)
 
-        gather_words(LAST, 2, 3, reuse="picked0_1")
-        gather_ts(2, 3, reuse="picked0_0")
+        gather_words(LAST, 2, 3)
+        gather_ts(2, 3, reuse="picked0_1")
         gather_words(LAST, 3, 4, reuse="picked_ts0")
 
         def direct_slice(s, first_bank, last_pieces):

@@ -180,7 +180,8 @@ def tile_list_tabts_gelu_kernel(tc, tab_words, tab_scales, w8, w4_words, w4_scal
             nc.scalar.activation(res[:, c0:c1], y[:, c0:c1], GELU, bias=bias[:, m : m + 1])
 
         gather_words(FIRST, 0, 4)
-        gather_ts(0, 2)
+        gather_ts(0, 1)
+        gather_ts(1, 2)
         ts_part = keep.tile([P, SLICE // P], F32, name="ts_part")
         picked_turned = bank(7)
         for i in range(SLICE // P):
@@ -223,7 +224,7 @@ def tile_list_tabts_gelu_kernel(tc, tab_words, tab_scales, w8, w4_words, w4_scal
 
         gather_words(LAST, 2, 3)
         gather_ts(2, 3, reuse="picked0_1")
-        gather_words(LAST, 3, 4, reuse="picked_ts0")
+        gather_words(LAST, 3, 4, reuse="picked_ts1")
 
         def direct_slice(s, first_bank, last_pieces):
             for m in range(ROW_TILES):

@@ -199,7 +199,12 @@ def tile_list_tabts_gelu_kernel(tc, tab_words, tab_scales, w8, w4_words, w4_scal
         nc.scalar.copy(w8_grouped[:], w8_raw[:].rearrange("p i n -> p n i"))
         nc.vector.quantize_mx(out=w8_codes[:].bitcast(FP8X4), scales=w8_plane[:], in_=w8_grouped[:].rearrange("p n i -> p (n i)"))
 
-        gather_words(LAST, 0, 1)
+        first_words = keep.tile([P, SLICE], U32, name="picked0_0", align_bytes=64)
+        for half in range(2):
+            cols = slice(half * SLICE // 2, (half + 1) * SLICE // 2)
+            window = table[LAST][:].bitcast(U32)
+            nc.vector.tensor_copy(first_words[:, cols], window.indirect(offsets[:, cols.start // 16 : cols.stop // 16]))
+        picked[LAST, 0] = first_words[:]
         gather_words(LAST, 1, 2)
         add_pass_slice0(LAST)
         add_pass_slice1(LAST)

@@ -25,7 +25,7 @@ HALF = S // 2
 ROW_TILES = M // P
 FIRST, SECOND, LAST = 2, 1, 0
 MOVES_AHEAD_OF_W8 = 6
-STORED_APART = 1
+STORED_APART = 4
 
 
 def tile_list_tabts_gelu_kernel(tc, tab_words, tab_scales, w8, w4_words, w4_scales, ts, b, offs, out):
@@ -132,10 +132,13 @@ def tile_list_tabts_gelu_kernel(tc, tab_words, tab_scales, w8, w4_words, w4_scal
             for s in range(s0, s1):
                 picked[a, s] = words[:, (s - s0) * SLICE : (s - s0 + 1) * SLICE]
 
-        def gather_ts(s0, s1, reuse=None):
+        def gather_ts(s0, s1, reuse=None, pieces=1):
             name = "picked_ts%d" % s0
             values = keep.tile([P, (s1 - s0) * SLICE], F32, name=name, tag=reuse or name, align_bytes=64)
-            nc.vector.tensor_copy(values[:], ts_win[:].indirect(entries(s0, s1)))
+            width = (s1 - s0) * SLICE // pieces
+            for c0 in range(0, (s1 - s0) * SLICE, width):
+                j0 = s0 * SLICE + c0
+                nc.vector.tensor_copy(values[:, c0 : c0 + width], ts_win[:].indirect(offsets[:, j0 // 16 : (j0 + width) // 16]))
             for s in range(s0, s1):
                 picked_ts[s] = values[:, (s - s0) * SLICE : (s - s0 + 1) * SLICE]
 
@@ -218,30 +221,50 @@ def tile_list_tabts_gelu_kernel(tc, tab_words, tab_scales, w8, w4_words, w4_scal
         scaled = keep.tile([P, SLICE // P, M], F32, name="scaled", align_bytes=64)
         for i in range(SLICE // P):
             nc.scalar.activation(scaled[:, i, :], turned_sums[i][:], COPY, scale=ts_part[:, i : i + 1])
-        for m in range(ROW_TILES):
+        gather_words(LAST, 2, 3)
+        sums = {}
+
+        def sum_direct(s, m, bank_no):
+            sums[s, m] = bank(bank_no)
+            for a in (FIRST, SECOND, LAST):
+                add_pass_direct(sums[s, m], a, s, m)
+
+        def finish_low(m, bank_no):
             finish_slice1(m)
-            back = bank(m)
+            back = bank(bank_no)
             for i in range(SLICE // P):
                 nc.tensor.transpose(back[:, i * P : (i + 1) * P], scaled[:, i, m * P : (m + 1) * P], ident[:])
             nc.scalar.activation(pairs[m][:, 0:SLICE], back[:], GELU, bias=bias[:, m : m + 1])
             width = SLICE if m < STORED_APART else HALF
             store(pairs[m][:, 0:width], m, 0, width)
 
-        gather_words(LAST, 2, 3)
+        def finish_high(s, m, pieces=1):
+            res = high[s][:, m, :]
+            width = SLICE // pieces
+            for c0 in range(0, SLICE, width):
+                finish_direct(sums[s, m], s, m, res, c0, c0 + width)
+                if (s, m) == (3, ROW_TILES - 1):
+                    store(res[:, c0 : c0 + width], m, s * SLICE + c0, s * SLICE + c0 + width)
+            if (s, m) != (3, ROW_TILES - 1):
+                store(res, m, s * SLICE, (s + 1) * SLICE)
+
+        sum_direct(2, 0, 0)
+        finish_low(0, 2)
+        finish_low(1, 3)
+        sum_direct(2, 1, 1)
+        finish_low(2, 4)
+        finish_low(3, 5)
+        high = {
+            2: keep.tile([P, ROW_TILES, SLICE], F32, name="res2", tag="scaled", align_bytes=64),
+            3: keep.tile([P, ROW_TILES, SLICE], F32, name="res3"),
+        }
         gather_ts(2, 3, reuse="picked0_1")
         gather_words(LAST, 3, 4, reuse="picked_ts1")
-
-        def direct_slice(s, first_bank, last_pieces):
-            for m in range(ROW_TILES):
-                acc = bank(first_bank + m)
-                for a in (FIRST, SECOND, LAST):
-                    add_pass_direct(acc, a, s, m)
-                res = keep.tile([P, SLICE], F32, name="res%d_%d" % (s, m))
-                width = SLICE // last_pieces if m == ROW_TILES - 1 else SLICE
-                for c0 in range(0, SLICE, width):
-                    finish_direct(acc, s, m, res, c0, c0 + width)
-                    store(res[:, c0 : c0 + width], m, s * SLICE + c0, s * SLICE + c0 + width)
-
-        direct_slice(2, 4, 1)
-        gather_ts(3, 4, reuse="y1_3_0")
-        direct_slice(3, 0, 2)
+        sum_direct(2, 2, 6)
+        sum_direct(2, 3, 7)
+        for m in range(ROW_TILES):
+            finish_high(2, m)
+        gather_ts(3, 4, reuse="picked0_2", pieces=2)
+        for m in range(ROW_TILES):
+            sum_direct(3, m, 2 + m)
+            finish_high(3, m, 2)

@@ -26,6 +26,7 @@ ROW_TILES = M // P
 FIRST, SECOND, LAST = 2, 1, 0
 MOVES_AHEAD_OF_W8 = 6
 STORED_APART = 4
+LATE = SLICE // 2
 
 
 def tile_list_tabts_gelu_kernel(tc, tab_words, tab_scales, w8, w4_words, w4_scales, ts, b, offs, out):
@@ -100,11 +101,12 @@ def tile_list_tabts_gelu_kernel(tc, tab_words, tab_scales, w8, w4_words, w4_scal
             for a in (FIRST, SECOND)
             for r in range(4)
         ]
-        early += [
-            (planes[4 + r : P : 32, 1:3, :].rearrange("p h w -> p (h w)"), picked_scales[112 + r : 128 : 4, :])
+        plane_last = keep.tile([P, 2, HALF // 4], I32, name="plane_last", tag="table%d" % FIRST, align_bytes=64)
+        late = [
+            (plane_last[r:P:32, :, :].rearrange("p h w -> p (h w)"), picked_scales[112 + r : 128 : 4, :])
             for r in range(4)
         ]
-        late = [(planes[32 * q : 32 * q + 4, 2:4, :], picked_scales[8 * q : 8 * q + 8, high_words]) for q in range(4)]
+        late += [(planes[32 * q : 32 * q + 4, 2:4, :], picked_scales[8 * q : 8 * q + 8, high_words]) for q in range(4)]
 
         def move_scales(moves):
             for plane_rows, picked_rows in moves:
@@ -115,7 +117,6 @@ def tile_list_tabts_gelu_kernel(tc, tab_words, tab_scales, w8, w4_words, w4_scal
         nc.sync.dma_start(w8_raw[:], w8.rearrange("(p i) n -> p i n", i=4))
         move_scales(early[MOVES_AHEAD_OF_W8:])
         load_table(LAST)
-        move_scales(late)
 
         picked = {}
         picked_ts = {}
@@ -148,13 +149,13 @@ def tile_list_tabts_gelu_kernel(tc, tab_words, tab_scales, w8, w4_words, w4_scal
             return w4[:, a - 1, 2 * n0 : 2 * n1].bitcast(FP4X4), w4_plane[:, a - 1, :].bitcast(U8)[:, n0:n1]
 
         def columns(a, s, j0, j1):
-            plane = planes[4 if a == 0 else 0 : P, block[a, s // 2], :].bitcast(U8)
+            plane = (plane_last[:, s // 2, :] if a == LAST else planes[:, block[a, s // 2], :]).bitcast(U8)
             start = (s % 2) * SLICE
             return picked[a, s][:, j0:j1].bitcast(FP8X4), plane[:, start + j0 : start + j1]
 
         def add_pass(acc, a, stationary, moving):
             nc.tensor.matmul_mx(
-                out=acc[:],
+                out=acc,
                 lhsT=stationary[0],
                 lhsT_scale=stationary[1],
                 rhs=moving[0],
@@ -164,11 +165,11 @@ def tile_list_tabts_gelu_kernel(tc, tab_words, tab_scales, w8, w4_words, w4_scal
             )
 
         def add_pass_direct(acc, a, s, m):
-            add_pass(acc, a, weights(a, m * P, (m + 1) * P), columns(a, s, 0, SLICE))
+            add_pass(acc[:], a, weights(a, m * P, (m + 1) * P), columns(a, s, 0, SLICE))
 
         def add_pass_slice0(a):
             for i in range(SLICE // P):
-                add_pass(turned_sums[i], a, columns(a, 0, i * P, (i + 1) * P), weights(a, 0, M))
+                add_pass(turned_sums[i][:], a, columns(a, 0, i * P, (i + 1) * P), weights(a, 0, M))
 
         def add_pass_slice1(a):
             for m in range(ROW_TILES):
@@ -183,6 +184,7 @@ def tile_list_tabts_gelu_kernel(tc, tab_words, tab_scales, w8, w4_words, w4_scal
             nc.scalar.activation(res[:, c0:c1], y[:, c0:c1], GELU, bias=bias[:, m : m + 1])
 
         gather_words(FIRST, 0, 4)
+        move_scales(late)
         gather_ts(0, 1)
         gather_ts(1, 2)
         ts_part = keep.tile([P, SLICE // P], F32, name="ts_part")
@@ -195,7 +197,9 @@ def tile_list_tabts_gelu_kernel(tc, tab_words, tab_scales, w8, w4_words, w4_scal
         add_pass_slice0(FIRST)
         add_pass_slice1(FIRST)
         gather_words(SECOND, 0, 2)
-        gather_words(SECOND, 2, 4)
+        second_high = keep.tile([P, HALF - LATE], U32, name="second_high", align_bytes=64)
+        nc.vector.tensor_copy(second_high[:], table[SECOND][:].bitcast(U32).indirect(offsets[:, HALF // 16 : (S - LATE) // 16]))
+        picked[SECOND, 2] = second_high[:, 0:SLICE]
         add_pass_slice0(SECOND)
         add_pass_slice1(SECOND)
         w8_grouped = keep.tile([P, M, 4], BF16, name="w8_grouped", align_bytes=64)
@@ -214,12 +218,20 @@ def tile_list_tabts_gelu_kernel(tc, tab_words, tab_scales, w8, w4_words, w4_scal
         pairs = [keep.tile([P, HALF], F32, name="pair%d" % m) for m in range(ROW_TILES)]
 
         def finish_slice1(m):
-            finish_direct(slice1_sums[m], 1, m, pairs[m][:, SLICE:HALF], 0, SLICE)
+            if m == 0:
+                nc.scalar.activation(pairs[m][:, SLICE:HALF], y_first[:], GELU, bias=bias[:, m : m + 1])
+            else:
+                finish_direct(slice1_sums[m], 1, m, pairs[m][:, SLICE:HALF], 0, SLICE)
             if m < STORED_APART:
                 store(pairs[m][:, SLICE:HALF], m, SLICE, HALF)
 
         scaled = keep.tile([P, SLICE // P, M], F32, name="scaled", align_bytes=64)
+        copied = keep.tile([P, SLICE], F32, name="copied", align_bytes=64)
+        y_first = keep.tile([P, SLICE], F32, name="y_first", align_bytes=64)
         for i in range(SLICE // P):
+            if i == SLICE // P - 1:
+                nc.scalar.copy(copied[:], slice1_sums[0][:])
+                nc.gpsimd.tensor_tensor(y_first[:], copied[:], picked_ts[1], MULT)
             nc.scalar.activation(scaled[:, i, :], turned_sums[i][:], COPY, scale=ts_part[:, i : i + 1])
         gather_words(LAST, 2, 3)
         sums = {}
@@ -227,7 +239,14 @@ def tile_list_tabts_gelu_kernel(tc, tab_words, tab_scales, w8, w4_words, w4_scal
         def sum_direct(s, m, bank_no):
             sums[s, m] = bank(bank_no)
             for a in (FIRST, SECOND, LAST):
-                add_pass_direct(sums[s, m], a, s, m)
+                if (a, s) == (SECOND, 3):
+                    plane = planes[:, block[a, 1], :].bitcast(U8)
+                    for words, c0 in ((second_high[:, SLICE : HALF - LATE], 0), (second_late[:], SLICE - LATE)):
+                        c1 = c0 + words.shape[1]
+                        moving = words.bitcast(FP8X4), plane[:, SLICE + c0 : SLICE + c1]
+                        add_pass(sums[s, m][:, c0:c1], a, weights(a, m * P, (m + 1) * P), moving)
+                else:
+                    add_pass_direct(sums[s, m], a, s, m)
 
         def finish_low(m, bank_no):
             finish_slice1(m)
@@ -259,6 +278,8 @@ def tile_list_tabts_gelu_kernel(tc, tab_words, tab_scales, w8, w4_words, w4_scal
             3: keep.tile([P, ROW_TILES, SLICE], F32, name="res3"),
         }
         gather_ts(2, 3, reuse="picked0_1")
+        second_late = keep.tile([P, LATE], U32, name="second_late", tag="copied", align_bytes=64)
+        nc.vector.tensor_copy(second_late[:], table[SECOND][:].bitcast(U32).indirect(offsets[:, (S - LATE) // 16 : S // 16]))
         gather_words(LAST, 3, 4, reuse="picked_ts1")
         sum_direct(2, 2, 6)
         sum_direct(2, 3, 7)

@@ -196,10 +196,11 @@ def tile_list_tabts_gelu_kernel(tc, tab_words, tab_scales, w8, w4_words, w4_scal
         slice1_sums = [bank(4 + m) for m in range(ROW_TILES)]
         add_pass_slice0(FIRST)
         add_pass_slice1(FIRST)
-        gather_words(SECOND, 0, 2)
+        gather_words(SECOND, 0, 1)
         second_high = keep.tile([P, HALF - LATE], U32, name="second_high", align_bytes=64)
         nc.vector.tensor_copy(second_high[:], table[SECOND][:].bitcast(U32).indirect(offsets[:, HALF // 16 : (S - LATE) // 16]))
         picked[SECOND, 2] = second_high[:, 0:SLICE]
+        gather_words(SECOND, 1, 2)
         add_pass_slice0(SECOND)
         add_pass_slice1(SECOND)
         w8_grouped = keep.tile([P, M, 4], BF16, name="w8_grouped", align_bytes=64)
@@ -268,8 +269,8 @@ def tile_list_tabts_gelu_kernel(tc, tab_words, tab_scales, w8, w4_words, w4_scal
                 store(res, m, s * SLICE, (s + 1) * SLICE)
 
         sum_direct(2, 0, 0)
-        finish_low(0, 2)
-        finish_low(1, 3)
+        finish_low(1, 2)
+        finish_low(0, 3)
         sum_direct(2, 1, 1)
         finish_low(2, 4)
         finish_low(3, 5)

@@ -26,7 +26,7 @@ ROW_TILES = M // P
 FIRST, SECOND, LAST = 2, 1, 0
 MOVES_AHEAD_OF_W8 = 6
 STORED_APART = 4
-LATE = SLICE // 2
+POOL_SHARE = 384
 
 
 def tile_list_tabts_gelu_kernel(tc, tab_words, tab_scales, w8, w4_words, w4_scales, ts, b, offs, out):
@@ -196,11 +196,8 @@ def tile_list_tabts_gelu_kernel(tc, tab_words, tab_scales, w8, w4_words, w4_scal
         slice1_sums = [bank(4 + m) for m in range(ROW_TILES)]
         add_pass_slice0(FIRST)
         add_pass_slice1(FIRST)
-        gather_words(SECOND, 0, 1)
-        second_high = keep.tile([P, HALF - LATE], U32, name="second_high", align_bytes=64)
-        nc.vector.tensor_copy(second_high[:], table[SECOND][:].bitcast(U32).indirect(offsets[:, HALF // 16 : (S - LATE) // 16]))
-        picked[SECOND, 2] = second_high[:, 0:SLICE]
-        gather_words(SECOND, 1, 2)
+        gather_words(SECOND, 0, 2)
+        gather_words(SECOND, 2, 4)
         add_pass_slice0(SECOND)
         add_pass_slice1(SECOND)
         w8_grouped = keep.tile([P, M, 4], BF16, name="w8_grouped", align_bytes=64)
@@ -220,6 +217,8 @@ def tile_list_tabts_gelu_kernel(tc, tab_words, tab_scales, w8, w4_words, w4_scal
 
         def finish_slice1(m):
             if m == 0:
+                rest = slice(POOL_SHARE, SLICE)
+                nc.vector.tensor_tensor(y_first[:, rest], slice1_sums[0][:, rest], picked_ts[1][:, rest], MULT)
                 nc.scalar.activation(pairs[m][:, SLICE:HALF], y_first[:], GELU, bias=bias[:, m : m + 1])
             else:
                 finish_direct(slice1_sums[m], 1, m, pairs[m][:, SLICE:HALF], 0, SLICE)
@@ -227,12 +226,12 @@ def tile_list_tabts_gelu_kernel(tc, tab_words, tab_scales, w8, w4_words, w4_scal
                 store(pairs[m][:, SLICE:HALF], m, SLICE, HALF)
 
         scaled = keep.tile([P, SLICE // P, M], F32, name="scaled", align_bytes=64)
-        copied = keep.tile([P, SLICE], F32, name="copied", align_bytes=64)
+        copied = keep.tile([P, POOL_SHARE], F32, name="copied", align_bytes=64)
         y_first = keep.tile([P, SLICE], F32, name="y_first", align_bytes=64)
         for i in range(SLICE // P):
             if i == SLICE // P - 1:
-                nc.scalar.copy(copied[:], slice1_sums[0][:])
-                nc.gpsimd.tensor_tensor(y_first[:], copied[:], picked_ts[1], MULT)
+                nc.scalar.copy(copied[:], slice1_sums[0][:, 0:POOL_SHARE])
+                nc.gpsimd.tensor_tensor(y_first[:, 0:POOL_SHARE], copied[:], picked_ts[1][:, 0:POOL_SHARE], MULT)
             nc.scalar.activation(scaled[:, i, :], turned_sums[i][:], COPY, scale=ts_part[:, i : i + 1])
         gather_words(LAST, 2, 3)
         sums = {}
@@ -240,14 +239,7 @@ def tile_list_tabts_gelu_kernel(tc, tab_words, tab_scales, w8, w4_words, w4_scal
         def sum_direct(s, m, bank_no):
             sums[s, m] = bank(bank_no)
             for a in (FIRST, SECOND, LAST):
-                if (a, s) == (SECOND, 3):
-                    plane = planes[:, block[a, 1], :].bitcast(U8)
-                    for words, c0 in ((second_high[:, SLICE : HALF - LATE], 0), (second_late[:], SLICE - LATE)):
-                        c1 = c0 + words.shape[1]
-                        moving = words.bitcast(FP8X4), plane[:, SLICE + c0 : SLICE + c1]
-                        add_pass(sums[s, m][:, c0:c1], a, weights(a, m * P, (m + 1) * P), moving)
-                else:
-                    add_pass_direct(sums[s, m], a, s, m)
+                add_pass_direct(sums[s, m], a, s, m)
 
         def finish_low(m, bank_no):
             finish_slice1(m)
@@ -279,8 +271,6 @@ def tile_list_tabts_gelu_kernel(tc, tab_words, tab_scales, w8, w4_words, w4_scal
             3: keep.tile([P, ROW_TILES, SLICE], F32, name="res3"),
         }
         gather_ts(2, 3, reuse="picked0_1")
-        second_late = keep.tile([P, LATE], U32, name="second_late", tag="copied", align_bytes=64)
-        nc.vector.tensor_copy(second_late[:], table[SECOND][:].bitcast(U32).indirect(offsets[:, (S - LATE) // 16 : S // 16]))
         gather_words(LAST, 3, 4, reuse="picked_ts1")
         sum_direct(2, 2, 6)
         sum_direct(2, 3, 7)

@@ -23,16 +23,18 @@ SLICE = 512
 SLICE_COLS = SLICE // 16
 HALF = S // 2
 ROW_TILES = M // P
-FIRST, SECOND, LAST = 2, 1, 0
-MOVES_AHEAD_OF_W8 = 6
+FIRST, SECOND, LAST = 1, 0, 2
+PLANE_ROW = {0: 4, 1: 0, 2: 0}
 STORED_APART = 4
-POOL_SHARE = 384
+LATE = 256
+POOL_SHARE = 512
 
 
 def tile_list_tabts_gelu_kernel(tc, tab_words, tab_scales, w8, w4_words, w4_scales, ts, b, offs, out):
     nc = tc.nc
     with ExitStack() as ctx:
         keep = ctx.enter_context(tc.tile_pool(name="keep", bufs=1))
+        placed = ctx.enter_context(tc.tile_pool(name="placed", bufs=1))
         psum = ctx.enter_context(tc.psum_pool(name="psum", bufs=1))
 
         def bank(i):
@@ -40,7 +42,7 @@ def tile_list_tabts_gelu_kernel(tc, tab_words, tab_scales, w8, w4_words, w4_scal
 
         offsets = keep.tile([P, S // 16], U16, name="offsets")
 
-        scale_win = keep.tile([P, T // 4], I32, name="scale_win", align_bytes=64)
+        scale_win = placed.tile([P, T // 4], I32, name="scale_win", offset=0, align_bytes=64)
         nc.gpsimd.memset(scale_win[64:112, :], 0)
         nc.vector.memset(scale_win[32:64, :], 0)
         nc.sync.dma_start(scale_win[0:32, :], tab_scales[1:3].rearrange("a n t -> n a t").bitcast(I32))
@@ -56,20 +58,22 @@ def tile_list_tabts_gelu_kernel(tc, tab_words, tab_scales, w8, w4_words, w4_scal
         warm = keep.tile([P, 1], F32, name="warm")
         nc.scalar.activation(warm[64:128, :], ts_rows[64:128, 0:1], GELU)
 
-        table = {a: keep.tile([P, T], I32, name="table%d" % a, align_bytes=64) for a in (FIRST, SECOND, LAST)}
+        table = {a: keep.tile([P, T], I32, name="table%d" % a, align_bytes=64) for a in (SECOND, LAST)}
+        table[FIRST] = placed.tile([P, T], I32, name="table_first", offset=T, align_bytes=64)
 
         def load_table(a):
             nc.sync.dma_start(table[a][:], tab_words[a].rearrange("p t i -> p (t i)").bitcast(I32))
 
         load_table(FIRST)
-        w4 = keep.tile([P, 2, 2 * M], U8, name="w4", align_bytes=64)
-        nc.sync.dma_start(w4[:].bitcast(I32), w4_words.rearrange("a p n -> p a n").bitcast(I32))
+        w4 = {a: keep.tile([P, 2 * M], U8, name="w4_%d" % a, align_bytes=64) for a in (FIRST, LAST)}
+        nc.sync.dma_start(w4[FIRST][:].bitcast(I32), w4_words[FIRST - 1].bitcast(I32))
         w4_plane = keep.tile([P, 2, M // 4], I32, name="w4_plane", align_bytes=64)
         nc.vector.memset(w4_plane[:], 0)
         for r in range(4):
             nc.sync.dma_start(w4_plane[r:P:32, :, :], w4_scales[:, r:16:4, :].rearrange("a q n -> q a n").bitcast(I32))
         nc.sync.dma_start(b_rows[0:ROW_TILES, :], b.rearrange("(m p) -> m p", p=P))
-        load_table(SECOND)
+        w8_raw = keep.tile([P, 4, M], F32, name="w8_raw")
+        nc.sync.dma_start(w8_raw[:], w8.rearrange("(p i) n -> p i n", i=4))
 
         ident = keep.tile([P, P], F32, name="ident")
         make_identity(nc, ident[:])
@@ -92,31 +96,29 @@ def tile_list_tabts_gelu_kernel(tc, tab_words, tab_scales, w8, w4_words, w4_scal
         picked_scales = keep.tile([P, S // 4], I32, name="picked_scales", align_bytes=64)
         nc.vector.tensor_copy(picked_scales[:].bitcast(U8), scale_win[:].bitcast(U8).indirect(offsets[:]))
 
-        planes = keep.tile([P, 4, HALF // 4], I32, name="planes", tag="scale_win", align_bytes=64)
-        block = {(2, 0): 0, (1, 0): 1, (1, 1): 2, (2, 1): 3, (0, 0): 1, (0, 1): 2}
         low_words = slice(0, HALF // 4)
         high_words = slice(HALF // 4, S // 4)
-        early = [
-            (planes[r:P:32, block[a, 0], :], picked_scales[2 * r + a - 1 : 32 : 8, low_words])
-            for a in (FIRST, SECOND)
-            for r in range(4)
-        ]
-        plane_last = keep.tile([P, 2, HALF // 4], I32, name="plane_last", tag="table%d" % FIRST, align_bytes=64)
-        late = [
-            (plane_last[r:P:32, :, :].rearrange("p h w -> p (h w)"), picked_scales[112 + r : 128 : 4, :])
-            for r in range(4)
-        ]
-        late += [(planes[32 * q : 32 * q + 4, 2:4, :], picked_scales[8 * q : 8 * q + 8, high_words]) for q in range(4)]
+        plane = {}
 
-        def move_scales(moves):
-            for plane_rows, picked_rows in moves:
-                nc.sync.dma_start(plane_rows, picked_rows)
+        def move_by_row(a, half, offset):
+            plane[a, half] = placed.tile([P, HALF // 4], I32, name="plane%d_%d" % (a, half), offset=offset, align_bytes=64)
+            for r in range(4):
+                rows = picked_scales[112 + r : 128 : 4, :] if a == 0 else picked_scales[2 * r + a - 1 : 32 : 8, :]
+                nc.sync.dma_start(plane[a, half][PLANE_ROW[a] + r : P : 32, :], rows[:, high_words if half else low_words])
 
-        move_scales(early[:MOVES_AHEAD_OF_W8])
-        w8_raw = keep.tile([P, 4, M], F32, name="w8_raw")
-        nc.sync.dma_start(w8_raw[:], w8.rearrange("(p i) n -> p i n", i=4))
-        move_scales(early[MOVES_AHEAD_OF_W8:])
+        move_by_row(FIRST, 0, 0)
+        load_table(SECOND)
+        move_by_row(SECOND, 0, HALF)
         load_table(LAST)
+        nc.sync.dma_start(w4[LAST][:].bitcast(I32), w4_words[LAST - 1].bitcast(I32))
+
+        def move_late():
+            move_by_row(LAST, 0, T)
+            both = placed.tile([P, 2, HALF // 4], I32, name="plane_high", offset=2 * HALF, align_bytes=64)
+            for q in range(4):
+                nc.sync.dma_start(both[32 * q : 32 * q + 4, :, :], picked_scales[8 * q : 8 * q + 8, high_words])
+            plane[1, 1], plane[2, 1] = both[:, 0, :], both[:, 1, :]
+            move_by_row(SECOND, 1, T + HALF)
 
         picked = {}
         picked_ts = {}
@@ -146,12 +148,12 @@ def tile_list_tabts_gelu_kernel(tc, tab_words, tab_scales, w8, w4_words, w4_scal
         def weights(a, n0, n1):
             if a == 0:
                 return w8_codes[:, n0:n1].bitcast(FP8X4), w8_plane[:, n0:n1]
-            return w4[:, a - 1, 2 * n0 : 2 * n1].bitcast(FP4X4), w4_plane[:, a - 1, :].bitcast(U8)[:, n0:n1]
+            return w4[a][:, 2 * n0 : 2 * n1].bitcast(FP4X4), w4_plane[:, a - 1, :].bitcast(U8)[:, n0:n1]
 
         def columns(a, s, j0, j1):
-            plane = (plane_last[:, s // 2, :] if a == LAST else planes[:, block[a, s // 2], :]).bitcast(U8)
+            rows = plane[a, s // 2][PLANE_ROW[a] : P, :].bitcast(U8)
             start = (s % 2) * SLICE
-            return picked[a, s][:, j0:j1].bitcast(FP8X4), plane[:, start + j0 : start + j1]
+            return picked[a, s][:, j0:j1].bitcast(FP8X4), rows[:, start + j0 : start + j1]
 
         def add_pass(acc, a, stationary, moving):
             nc.tensor.matmul_mx(
@@ -184,7 +186,7 @@ def tile_list_tabts_gelu_kernel(tc, tab_words, tab_scales, w8, w4_words, w4_scal
             nc.scalar.activation(res[:, c0:c1], y[:, c0:c1], GELU, bias=bias[:, m : m + 1])
 
         gather_words(FIRST, 0, 4)
-        move_scales(late)
+        move_late()
         gather_ts(0, 1)
         gather_ts(1, 2)
         ts_part = keep.tile([P, SLICE // P], F32, name="ts_part")
@@ -196,15 +198,17 @@ def tile_list_tabts_gelu_kernel(tc, tab_words, tab_scales, w8, w4_words, w4_scal
         slice1_sums = [bank(4 + m) for m in range(ROW_TILES)]
         add_pass_slice0(FIRST)
         add_pass_slice1(FIRST)
-        gather_words(SECOND, 0, 2)
-        gather_words(SECOND, 2, 4)
-        add_pass_slice0(SECOND)
-        add_pass_slice1(SECOND)
         w8_grouped = keep.tile([P, M, 4], BF16, name="w8_grouped", align_bytes=64)
         nc.scalar.copy(w8_grouped[:], w8_raw[:].rearrange("p i n -> p n i"))
         nc.vector.quantize_mx(out=w8_codes[:].bitcast(FP8X4), scales=w8_plane[:], in_=w8_grouped[:].rearrange("p n i -> p (n i)"))
+        gather_words(SECOND, 0, 2)
+        second_high = keep.tile([P, HALF - LATE], U32, name="second_high", align_bytes=64)
+        nc.vector.tensor_copy(second_high[:], table[SECOND][:].bitcast(U32).indirect(offsets[:, HALF // 16 : (S - LATE) // 16]))
+        picked[SECOND, 2] = second_high[:, 0:SLICE]
+        add_pass_slice0(SECOND)
+        add_pass_slice1(SECOND)
 
-        first_words = keep.tile([P, SLICE], U32, name="picked0_0", align_bytes=64)
+        first_words = keep.tile([P, SLICE], U32, name="picked2_0", align_bytes=64)
         for half in range(2):
             cols = slice(half * SLICE // 2, (half + 1) * SLICE // 2)
             window = table[LAST][:].bitcast(U32)
@@ -217,8 +221,6 @@ def tile_list_tabts_gelu_kernel(tc, tab_words, tab_scales, w8, w4_words, w4_scal
 
         def finish_slice1(m):
             if m == 0:
-                rest = slice(POOL_SHARE, SLICE)
-                nc.vector.tensor_tensor(y_first[:, rest], slice1_sums[0][:, rest], picked_ts[1][:, rest], MULT)
                 nc.scalar.activation(pairs[m][:, SLICE:HALF], y_first[:], GELU, bias=bias[:, m : m + 1])
             else:
                 finish_direct(slice1_sums[m], 1, m, pairs[m][:, SLICE:HALF], 0, SLICE)
@@ -239,7 +241,14 @@ def tile_list_tabts_gelu_kernel(tc, tab_words, tab_scales, w8, w4_words, w4_scal
         def sum_direct(s, m, bank_no):
             sums[s, m] = bank(bank_no)
             for a in (FIRST, SECOND, LAST):
-                add_pass_direct(sums[s, m], a, s, m)
+                if (a, s) == (SECOND, 3):
+                    rows = plane[a, 1][PLANE_ROW[a] : P, :].bitcast(U8)
+                    for j0, words in ((0, second_high[:, SLICE : HALF - LATE]), (SLICE - LATE, second_late[:])):
+                        j1 = j0 + words.shape[1]
+                        moving = (words.bitcast(FP8X4), rows[:, SLICE + j0 : SLICE + j1])
+                        add_pass(sums[s, m][:, j0:j1], a, weights(a, m * P, (m + 1) * P), moving)
+                else:
+                    add_pass_direct(sums[s, m], a, s, m)
 
         def finish_low(m, bank_no):
             finish_slice1(m)
@@ -270,13 +279,15 @@ def tile_list_tabts_gelu_kernel(tc, tab_words, tab_scales, w8, w4_words, w4_scal
             2: keep.tile([P, ROW_TILES, SLICE], F32, name="res2", tag="scaled", align_bytes=64),
             3: keep.tile([P, ROW_TILES, SLICE], F32, name="res3"),
         }
-        gather_ts(2, 3, reuse="picked0_1")
+        gather_ts(2, 3, reuse="picked2_1")
         gather_words(LAST, 3, 4, reuse="picked_ts1")
+        second_late = keep.tile([P, LATE], U32, name="second_late", tag="copied", align_bytes=64)
+        nc.vector.tensor_copy(second_late[:], table[SECOND][:].bitcast(U32).indirect(offsets[:, (S - LATE) // 16 : S // 16]))
         sum_direct(2, 2, 6)
         sum_direct(2, 3, 7)
         for m in range(ROW_TILES):
             finish_high(2, m)
-        gather_ts(3, 4, reuse="picked0_2", pieces=2)
+        gather_ts(3, 4, reuse="picked2_2", pieces=2)
         for m in range(ROW_TILES):
             sum_direct(3, m, 2 + m)
             finish_high(3, m, 2)

@@ -96,29 +96,30 @@ def tile_list_tabts_gelu_kernel(tc, tab_words, tab_scales, w8, w4_words, w4_scal
         picked_scales = keep.tile([P, S // 4], I32, name="picked_scales", align_bytes=64)
         nc.vector.tensor_copy(picked_scales[:].bitcast(U8), scale_win[:].bitcast(U8).indirect(offsets[:]))
 
-        low_words = slice(0, HALF // 4)
         high_words = slice(HALF // 4, S // 4)
         plane = {}
 
-        def move_by_row(a, half, offset):
-            plane[a, half] = placed.tile([P, HALF // 4], I32, name="plane%d_%d" % (a, half), offset=offset, align_bytes=64)
+        def move_by_row(a, halves, offset):
+            width = halves * HALF // 4
+            moved = placed.tile([P, width], I32, name="plane%d" % a, offset=offset, align_bytes=64)
             for r in range(4):
                 rows = picked_scales[112 + r : 128 : 4, :] if a == 0 else picked_scales[2 * r + a - 1 : 32 : 8, :]
-                nc.sync.dma_start(plane[a, half][PLANE_ROW[a] + r : P : 32, :], rows[:, high_words if half else low_words])
+                nc.sync.dma_start(moved[PLANE_ROW[a] + r : P : 32, :], rows[:, 0:width])
+            for half in range(halves):
+                plane[a, half] = moved[:, half * HALF // 4 : (half + 1) * HALF // 4]
 
-        move_by_row(FIRST, 0, 0)
+        move_by_row(FIRST, 1, 0)
         load_table(SECOND)
-        move_by_row(SECOND, 0, HALF)
+        move_by_row(SECOND, 2, HALF)
         load_table(LAST)
         nc.sync.dma_start(w4[LAST][:].bitcast(I32), w4_words[LAST - 1].bitcast(I32))
 
         def move_late():
-            move_by_row(LAST, 0, T)
-            both = placed.tile([P, 2, HALF // 4], I32, name="plane_high", offset=2 * HALF, align_bytes=64)
+            move_by_row(LAST, 1, T)
+            both = placed.tile([P, 2, HALF // 4], I32, name="plane_high", offset=T + HALF, align_bytes=64)
             for q in range(4):
                 nc.sync.dma_start(both[32 * q : 32 * q + 4, :, :], picked_scales[8 * q : 8 * q + 8, high_words])
             plane[1, 1], plane[2, 1] = both[:, 0, :], both[:, 1, :]
-            move_by_row(SECOND, 1, T + HALF)
 
         picked = {}
         picked_ts = {}

@@ -27,7 +27,8 @@ FIRST, SECOND, LAST = 1, 0, 2
 PLANE_ROW = {0: 4, 1: 0, 2: 0}
 STORED_APART = 4
 LATE = 256
-POOL_SHARE = 512
+POOL_SHARE2 = 512
+POOL_SHARE = 256
 
 
 def tile_list_tabts_gelu_kernel(tc, tab_words, tab_scales, w8, w4_words, w4_scales, ts, b, offs, out):
@@ -96,30 +97,30 @@ def tile_list_tabts_gelu_kernel(tc, tab_words, tab_scales, w8, w4_words, w4_scal
         picked_scales = keep.tile([P, S // 4], I32, name="picked_scales", align_bytes=64)
         nc.vector.tensor_copy(picked_scales[:].bitcast(U8), scale_win[:].bitcast(U8).indirect(offsets[:]))
 
-        high_words = slice(HALF // 4, S // 4)
         plane = {}
 
-        def move_by_row(a, halves, offset):
-            width = halves * HALF // 4
-            moved = placed.tile([P, width], I32, name="plane%d" % a, offset=offset, align_bytes=64)
-            for r in range(4):
-                rows = picked_scales[112 + r : 128 : 4, :] if a == 0 else picked_scales[2 * r + a - 1 : 32 : 8, :]
-                nc.sync.dma_start(moved[PLANE_ROW[a] + r : P : 32, :], rows[:, 0:width])
-            for half in range(halves):
-                plane[a, half] = moved[:, half * HALF // 4 : (half + 1) * HALF // 4]
+        def move_e2m1_partners(half, offset):
+            both = placed.tile([P, 2, HALF // 4], I32, name="planes12_%d" % half, offset=offset, align_bytes=64)
+            words = slice(half * HALF // 4, (half + 1) * HALF // 4)
+            for q in (0, 2, 1, 3):
+                nc.sync.dma_start(both[32 * q : 32 * q + 4, :, :], picked_scales[8 * q : 8 * q + 8, words])
+            plane[1, half], plane[2, half] = both[:, 0, :], both[:, 1, :]
 
-        move_by_row(FIRST, 1, 0)
+        def move_pass0(half, offset):
+            plane[0, half] = placed.tile([P, HALF // 4], I32, name="plane0_%d" % half, offset=offset, align_bytes=64)
+            words = slice(half * HALF // 4, (half + 1) * HALF // 4)
+            for r in range(4):
+                nc.sync.dma_start(plane[0, half][PLANE_ROW[0] + r : P : 32, :], picked_scales[112 + r : 128 : 4, words])
+
+        move_e2m1_partners(0, 0)
         load_table(SECOND)
-        move_by_row(SECOND, 2, HALF)
+        move_pass0(0, S)
         load_table(LAST)
         nc.sync.dma_start(w4[LAST][:].bitcast(I32), w4_words[LAST - 1].bitcast(I32))
 
         def move_late():
-            move_by_row(LAST, 1, T)
-            both = placed.tile([P, 2, HALF // 4], I32, name="plane_high", offset=T + HALF, align_bytes=64)
-            for q in range(4):
-                nc.sync.dma_start(both[32 * q : 32 * q + 4, :, :], picked_scales[8 * q : 8 * q + 8, high_words])
-            plane[1, 1], plane[2, 1] = both[:, 0, :], both[:, 1, :]
+            move_e2m1_partners(1, T)
+            move_pass0(1, T + S)
 
         picked = {}
         picked_ts = {}
@@ -222,6 +223,8 @@ def tile_list_tabts_gelu_kernel(tc, tab_words, tab_scales, w8, w4_words, w4_scal
 
         def finish_slice1(m):
             if m == 0:
+                rest = slice(POOL_SHARE, SLICE)
+                nc.vector.tensor_tensor(y_first[:, rest], slice1_sums[0][:, rest], picked_ts[1][:, rest], MULT)
                 nc.scalar.activation(pairs[m][:, SLICE:HALF], y_first[:], GELU, bias=bias[:, m : m + 1])
             else:
                 finish_direct(slice1_sums[m], 1, m, pairs[m][:, SLICE:HALF], 0, SLICE)
@@ -274,20 +277,27 @@ def tile_list_tabts_gelu_kernel(tc, tab_words, tab_scales, w8, w4_words, w4_scal
         finish_low(1, 2)
         finish_low(0, 3)
         sum_direct(2, 1, 1)
+        copied2 = keep.tile([P, POOL_SHARE2], F32, name="copied2", align_bytes=64)
+        nc.scalar.copy(copied2[:], sums[2, 0][:, 0:POOL_SHARE2])
         finish_low(2, 4)
         finish_low(3, 5)
         high = {
             2: keep.tile([P, ROW_TILES, SLICE], F32, name="res2", tag="scaled", align_bytes=64),
-            3: keep.tile([P, ROW_TILES, SLICE], F32, name="res3"),
         }
         gather_ts(2, 3, reuse="picked2_1")
-        gather_words(LAST, 3, 4, reuse="picked_ts1")
         second_late = keep.tile([P, LATE], U32, name="second_late", tag="copied", align_bytes=64)
         nc.vector.tensor_copy(second_late[:], table[SECOND][:].bitcast(U32).indirect(offsets[:, (S - LATE) // 16 : S // 16]))
+        gather_words(LAST, 3, 4, reuse="picked_ts1")
         sum_direct(2, 2, 6)
         sum_direct(2, 3, 7)
-        for m in range(ROW_TILES):
-            finish_high(2, m)
+        y_second = keep.tile([P, POOL_SHARE2], F32, name="y_second", tag="table%d" % LAST, align_bytes=64)
+        nc.gpsimd.tensor_tensor(y_second[:], copied2[:], picked_ts[2][:, 0:POOL_SHARE2], MULT)
+        finish_high(2, 1)
+        finish_high(2, 2)
+        nc.scalar.activation(high[2][:, 0, 0:POOL_SHARE2], y_second[:], GELU, bias=bias[:, 0:1])
+        store(high[2][:, 0, :], 0, 2 * SLICE, 3 * SLICE)
+        finish_high(2, 3)
+        high[3] = keep.tile([P, ROW_TILES, SLICE], F32, name="res3", tag="table%d" % LAST, align_bytes=64)
         gather_ts(3, 4, reuse="picked2_2", pieces=2)
         for m in range(ROW_TILES):
             sum_direct(3, m, 2 + m)

@@ -28,7 +28,7 @@ PLANE_ROW = {0: 4, 1: 0, 2: 0}
 STORED_APART = 4
 LATE = 256
 POOL_SHARE2 = 512
-POOL_SHARE = 256
+POOL_SHARE = 192
 
 
 def tile_list_tabts_gelu_kernel(tc, tab_words, tab_scales, w8, w4_words, w4_scales, ts, b, offs, out):
@@ -180,7 +180,8 @@ def tile_list_tabts_gelu_kernel(tc, tab_words, tab_scales, w8, w4_words, w4_scal
                 add_pass_direct(slice1_sums[m], a, 1, m)
 
         def store(res, m, j0, j1):
-            nc.sync.dma_start(out[m * P : (m + 1) * P, j0:j1], res)
+            queue = nc.scalar if (m, j1) == (ROW_TILES - 1, S) else nc.sync
+            queue.dma_start(out[m * P : (m + 1) * P, j0:j1], res)
 
         def finish_direct(acc, s, m, res, c0, c1):
             y = keep.tile([P, SLICE], F32, name="y%d_%d_%d" % (s, m, c0), align_bytes=64)
@@ -297,7 +298,7 @@ def tile_list_tabts_gelu_kernel(tc, tab_words, tab_scales, w8, w4_words, w4_scal
         nc.scalar.activation(high[2][:, 0, 0:POOL_SHARE2], y_second[:], GELU, bias=bias[:, 0:1])
         store(high[2][:, 0, :], 0, 2 * SLICE, 3 * SLICE)
         finish_high(2, 3)
-        high[3] = keep.tile([P, ROW_TILES, SLICE], F32, name="res3", tag="table%d" % LAST, align_bytes=64)
+        high[3] = keep.tile([P, ROW_TILES, SLICE], F32, name="res3", align_bytes=64)
         gather_ts(3, 4, reuse="picked2_2", pieces=2)
         for m in range(ROW_TILES):
             sum_direct(3, m, 2 + m)

@@ -180,8 +180,7 @@ def tile_list_tabts_gelu_kernel(tc, tab_words, tab_scales, w8, w4_words, w4_scal
                 add_pass_direct(slice1_sums[m], a, 1, m)
 
         def store(res, m, j0, j1):
-            queue = nc.scalar if (m, j1) == (ROW_TILES - 1, S) else nc.sync
-            queue.dma_start(out[m * P : (m + 1) * P, j0:j1], res)
+            nc.sync.dma_start(out[m * P : (m + 1) * P, j0:j1], res)
 
         def finish_direct(acc, s, m, res, c0, c1):
             y = keep.tile([P, SLICE], F32, name="y%d_%d_%d" % (s, m, c0), align_bytes=64)

from contextlib import ExitStack

import concourse.mybir as mybir
from concourse.masks import make_identity

K, M, T, S = 1536, 512, 4096, 2048
FLOPS = 2 * K * M * S

F32 = mybir.dt.float32
BF16 = mybir.dt.bfloat16
I32 = mybir.dt.int32
U32 = mybir.dt.uint32
U16 = mybir.dt.uint16
U8 = mybir.dt.uint8
FP8X4 = mybir.dt.float8_e4m3fn_x4
FP4X4 = mybir.dt.float4_e2m1fn_x4
GELU = mybir.ActivationFunctionType.Gelu_apprx_tanh
COPY = mybir.ActivationFunctionType.Copy
MULT = mybir.AluOpType.mult

P = 128
SLICE = 512
SLICE_COLS = SLICE // 16
HALF = S // 2
ROW_TILES = M // P
FIRST, SECOND, LAST = 1, 0, 2
PLANE_ROW = {0: 4, 1: 0, 2: 0}
STORED_APART = 4
LATE = 256
POOL_SHARE2 = 512
POOL_SHARE = 192


def tile_list_tabts_gelu_kernel(tc, tab_words, tab_scales, w8, w4_words, w4_scales, ts, b, offs, out):
    nc = tc.nc
    with ExitStack() as ctx:
        keep = ctx.enter_context(tc.tile_pool(name="keep", bufs=1))
        placed = ctx.enter_context(tc.tile_pool(name="placed", bufs=1))
        psum = ctx.enter_context(tc.psum_pool(name="psum", bufs=1))

        def bank(i):
            return psum.tile([P, SLICE], F32, name="bank%d" % i, tag="bank%d" % i)

        offsets = keep.tile([P, S // 16], U16, name="offsets")

        scale_win = placed.tile([P, T // 4], I32, name="scale_win", offset=0, align_bytes=64)
        nc.gpsimd.memset(scale_win[64:112, :], 0)
        nc.vector.memset(scale_win[32:64, :], 0)
        nc.sync.dma_start(scale_win[0:32, :], tab_scales[1:3].rearrange("a n t -> n a t").bitcast(I32))
        nc.sync.dma_start(offsets[:], offs)
        ts_rows = keep.tile([P, P], F32, name="ts_rows")
        nc.sync.dma_start(ts_rows[0:32, :], ts[0].rearrange("(c p) -> c p", p=P))
        nc.scalar.dma_start(scale_win[112:128, :], tab_scales[0].bitcast(I32))
        nc.vector.memset(ts_rows[32:64, :], 0.0)
        nc.vector.memset(ts_rows[64:128, :], 0.0)
        b_rows = keep.tile([P, P], F32, name="b_rows")
        nc.vector.memset(b_rows[:], 0.0)

        warm = keep.tile([P, 1], F32, name="warm")
        nc.scalar.activation(warm[64:128, :], ts_rows[64:128, 0:1], GELU)

        table = {a: keep.tile([P, T], I32, name="table%d" % a, align_bytes=64) for a in (SECOND, LAST)}
        table[FIRST] = placed.tile([P, T], I32, name="table_first", offset=T, align_bytes=64)

        def load_table(a):
            nc.sync.dma_start(table[a][:], tab_words[a].rearrange("p t i -> p (t i)").bitcast(I32))

        load_table(FIRST)
        w4 = {a: keep.tile([P, 2 * M], U8, name="w4_%d" % a, align_bytes=64) for a in (FIRST, LAST)}
        nc.sync.dma_start(w4[FIRST][:].bitcast(I32), w4_words[FIRST - 1].bitcast(I32))
        w4_plane = keep.tile([P, 2, M // 4], I32, name="w4_plane", align_bytes=64)
        nc.vector.memset(w4_plane[:], 0)
        for r in range(4):
            nc.sync.dma_start(w4_plane[r:P:32, :, :], w4_scales[:, r:16:4, :].rearrange("a q n -> q a n").bitcast(I32))
        nc.sync.dma_start(b_rows[0:ROW_TILES, :], b.rearrange("(m p) -> m p", p=P))
        w8_raw = keep.tile([P, 4, M], F32, name="w8_raw")
        nc.sync.dma_start(w8_raw[:], w8.rearrange("(p i) n -> p i n", i=4))

        ident = keep.tile([P, P], F32, name="ident")
        make_identity(nc, ident[:])
        ts_cols = keep.tile([P, T // P], F32, name="ts_cols")
        ts_turned = bank(0)
        nc.tensor.transpose(ts_turned[:, 0:P], ts_rows[:], ident[:])
        nc.scalar.copy(ts_cols[:], ts_turned[:, 0 : T // P])
        ts_win = keep.tile([P, T], F32, name="ts_win", align_bytes=64)
        for g in range(T // SLICE):
            spread = bank(1 + g % 4)
            for c in range(4):
                col = 4 * g + c
                nc.tensor.transpose(spread[:, c * P : (c + 1) * P], ts_cols[:, col : col + 1].to_broadcast([P, P]), ident[:])
            nc.scalar.copy(ts_win[:, g * SLICE : (g + 1) * SLICE], spread[:])
        bias = keep.tile([P, ROW_TILES], F32, name="bias")
        b_turned = bank(5)
        nc.tensor.transpose(b_turned[:, 0:P], b_rows[:], ident[:])
        nc.scalar.copy(bias[:], b_turned[:, 0:ROW_TILES])

        picked_scales = keep.tile([P, S // 4], I32, name="picked_scales", align_bytes=64)
        nc.vector.tensor_copy(picked_scales[:].bitcast(U8), scale_win[:].bitcast(U8).indirect(offsets[:]))

        plane = {}

        def move_e2m1_partners(half, offset):
            both = placed.tile([P, 2, HALF // 4], I32, name="planes12_%d" % half, offset=offset, align_bytes=64)
            words = slice(half * HALF // 4, (half + 1) * HALF // 4)
            for q in (0, 2, 1, 3):
                nc.sync.dma_start(both[32 * q : 32 * q + 4, :, :], picked_scales[8 * q : 8 * q + 8, words])
            plane[1, half], plane[2, half] = both[:, 0, :], both[:, 1, :]

        def move_pass0(half, offset):
            plane[0, half] = placed.tile([P, HALF // 4], I32, name="plane0_%d" % half, offset=offset, align_bytes=64)
            words = slice(half * HALF // 4, (half + 1) * HALF // 4)
            for r in range(4):
                nc.sync.dma_start(plane[0, half][PLANE_ROW[0] + r : P : 32, :], picked_scales[112 + r : 128 : 4, words])

        move_e2m1_partners(0, 0)
        load_table(SECOND)
        move_pass0(0, S)
        load_table(LAST)
        nc.sync.dma_start(w4[LAST][:].bitcast(I32), w4_words[LAST - 1].bitcast(I32))

        def move_late():
            move_e2m1_partners(1, T)
            move_pass0(1, T + S)

        picked = {}
        picked_ts = {}
        w8_codes = keep.tile([P, M], U32, name="w8_codes", align_bytes=64)
        w8_plane = keep.tile([P, M], U8, name="w8_plane", align_bytes=64)

        def entries(s0, s1):
            return offsets[:, s0 * SLICE_COLS : s1 * SLICE_COLS]

        def gather_words(a, s0, s1, reuse=None):
            name = "picked%d_%d" % (a, s0)
            words = keep.tile([P, (s1 - s0) * SLICE], U32, name=name, tag=reuse or name, align_bytes=64)
            nc.vector.tensor_copy(words[:], table[a][:].bitcast(U32).indirect(entries(s0, s1)))
            for s in range(s0, s1):
                picked[a, s] = words[:, (s - s0) * SLICE : (s - s0 + 1) * SLICE]

        def gather_ts(s0, s1, reuse=None, pieces=1):
            name = "picked_ts%d" % s0
            values = keep.tile([P, (s1 - s0) * SLICE], F32, name=name, tag=reuse or name, align_bytes=64)
            width = (s1 - s0) * SLICE // pieces
            for c0 in range(0, (s1 - s0) * SLICE, width):
                j0 = s0 * SLICE + c0
                nc.vector.tensor_copy(values[:, c0 : c0 + width], ts_win[:].indirect(offsets[:, j0 // 16 : (j0 + width) // 16]))
            for s in range(s0, s1):
                picked_ts[s] = values[:, (s - s0) * SLICE : (s - s0 + 1) * SLICE]

        def weights(a, n0, n1):
            if a == 0:
                return w8_codes[:, n0:n1].bitcast(FP8X4), w8_plane[:, n0:n1]
            return w4[a][:, 2 * n0 : 2 * n1].bitcast(FP4X4), w4_plane[:, a - 1, :].bitcast(U8)[:, n0:n1]

        def columns(a, s, j0, j1):
            rows = plane[a, s // 2][PLANE_ROW[a] : P, :].bitcast(U8)
            start = (s % 2) * SLICE
            return picked[a, s][:, j0:j1].bitcast(FP8X4), rows[:, start + j0 : start + j1]

        def add_pass(acc, a, stationary, moving):
            nc.tensor.matmul_mx(
                out=acc,
                lhsT=stationary[0],
                lhsT_scale=stationary[1],
                rhs=moving[0],
                rhs_scale=moving[1],
                start=(a == FIRST),
                stop=(a == LAST),
            )

        def add_pass_direct(acc, a, s, m):
            add_pass(acc[:], a, weights(a, m * P, (m + 1) * P), columns(a, s, 0, SLICE))

        def add_pass_slice0(a):
            for i in range(SLICE // P):
                add_pass(turned_sums[i][:], a, columns(a, 0, i * P, (i + 1) * P), weights(a, 0, M))

        def add_pass_slice1(a):
            for m in range(ROW_TILES):
                add_pass_direct(slice1_sums[m], a, 1, m)

        def store(res, m, j0, j1):
            nc.sync.dma_start(out[m * P : (m + 1) * P, j0:j1], res)

        def finish_direct(acc, s, m, res, c0, c1):
            y = keep.tile([P, SLICE], F32, name="y%d_%d_%d" % (s, m, c0), align_bytes=64)
            nc.vector.tensor_tensor(y[:, c0:c1], acc[:, c0:c1], picked_ts[s][:, c0:c1], MULT)
            nc.scalar.activation(res[:, c0:c1], y[:, c0:c1], GELU, bias=bias[:, m : m + 1])

        gather_words(FIRST, 0, 4)
        move_late()
        gather_ts(0, 1)
        gather_ts(1, 2)
        ts_part = keep.tile([P, SLICE // P], F32, name="ts_part")
        picked_turned = bank(7)
        for i in range(SLICE // P):
            nc.tensor.transpose(picked_turned[:, i * P : (i + 1) * P], picked_ts[0][:, i * P : (i + 1) * P], ident[:])
        nc.scalar.copy(ts_part[:], picked_turned[:, 0:SLICE:P])
        turned_sums = [bank(i) for i in range(SLICE // P)]
        slice1_sums = [bank(4 + m) for m in range(ROW_TILES)]
        add_pass_slice0(FIRST)
        add_pass_slice1(FIRST)
        w8_grouped = keep.tile([P, M, 4], BF16, name="w8_grouped", align_bytes=64)
        nc.scalar.copy(w8_grouped[:], w8_raw[:].rearrange("p i n -> p n i"))
        nc.vector.quantize_mx(out=w8_codes[:].bitcast(FP8X4), scales=w8_plane[:], in_=w8_grouped[:].rearrange("p n i -> p (n i)"))
        gather_words(SECOND, 0, 2)
        second_high = keep.tile([P, HALF - LATE], U32, name="second_high", align_bytes=64)
        nc.vector.tensor_copy(second_high[:], table[SECOND][:].bitcast(U32).indirect(offsets[:, HALF // 16 : (S - LATE) // 16]))
        picked[SECOND, 2] = second_high[:, 0:SLICE]
        add_pass_slice0(SECOND)
        add_pass_slice1(SECOND)

        first_words = keep.tile([P, SLICE], U32, name="picked2_0", align_bytes=64)
        for half in range(2):
            cols = slice(half * SLICE // 2, (half + 1) * SLICE // 2)
            window = table[LAST][:].bitcast(U32)
            nc.vector.tensor_copy(first_words[:, cols], window.indirect(offsets[:, cols.start // 16 : cols.stop // 16]))
        picked[LAST, 0] = first_words[:]
        gather_words(LAST, 1, 2)
        add_pass_slice0(LAST)
        add_pass_slice1(LAST)
        pairs = [keep.tile([P, HALF], F32, name="pair%d" % m) for m in range(ROW_TILES)]

        def finish_slice1(m):
            if m == 0:
                rest = slice(POOL_SHARE, SLICE)
                nc.vector.tensor_tensor(y_first[:, rest], slice1_sums[0][:, rest], picked_ts[1][:, rest], MULT)
                nc.scalar.activation(pairs[m][:, SLICE:HALF], y_first[:], GELU, bias=bias[:, m : m + 1])
            else:
                finish_direct(slice1_sums[m], 1, m, pairs[m][:, SLICE:HALF], 0, SLICE)
            if m < STORED_APART:
                store(pairs[m][:, SLICE:HALF], m, SLICE, HALF)

        scaled = keep.tile([P, SLICE // P, M], F32, name="scaled", align_bytes=64)
        copied = keep.tile([P, POOL_SHARE], F32, name="copied", align_bytes=64)
        y_first = keep.tile([P, SLICE], F32, name="y_first", align_bytes=64)
        for i in range(SLICE // P):
            if i == SLICE // P - 1:
                nc.scalar.copy(copied[:], slice1_sums[0][:, 0:POOL_SHARE])
                nc.gpsimd.tensor_tensor(y_first[:, 0:POOL_SHARE], copied[:], picked_ts[1][:, 0:POOL_SHARE], MULT)
            nc.scalar.activation(scaled[:, i, :], turned_sums[i][:], COPY, scale=ts_part[:, i : i + 1])
        gather_words(LAST, 2, 3)
        sums = {}

        def sum_direct(s, m, bank_no):
            sums[s, m] = bank(bank_no)
            for a in (FIRST, SECOND, LAST):
                if (a, s) == (SECOND, 3):
                    rows = plane[a, 1][PLANE_ROW[a] : P, :].bitcast(U8)
                    for j0, words in ((0, second_high[:, SLICE : HALF - LATE]), (SLICE - LATE, second_late[:])):
                        j1 = j0 + words.shape[1]
                        moving = (words.bitcast(FP8X4), rows[:, SLICE + j0 : SLICE + j1])
                        add_pass(sums[s, m][:, j0:j1], a, weights(a, m * P, (m + 1) * P), moving)
                else:
                    add_pass_direct(sums[s, m], a, s, m)

        def finish_low(m, bank_no):
            finish_slice1(m)
            back = bank(bank_no)
            for i in range(SLICE // P):
                nc.tensor.transpose(back[:, i * P : (i + 1) * P], scaled[:, i, m * P : (m + 1) * P], ident[:])
            nc.scalar.activation(pairs[m][:, 0:SLICE], back[:], GELU, bias=bias[:, m : m + 1])
            width = SLICE if m < STORED_APART else HALF
            store(pairs[m][:, 0:width], m, 0, width)

        def finish_high(s, m, pieces=1):
            res = high[s][:, m, :]
            width = SLICE // pieces
            for c0 in range(0, SLICE, width):
                finish_direct(sums[s, m], s, m, res, c0, c0 + width)
                if (s, m) == (3, ROW_TILES - 1):
                    store(res[:, c0 : c0 + width], m, s * SLICE + c0, s * SLICE + c0 + width)
            if (s, m) != (3, ROW_TILES - 1):
                store(res, m, s * SLICE, (s + 1) * SLICE)

        sum_direct(2, 0, 0)
        finish_low(1, 2)
        finish_low(0, 3)
        sum_direct(2, 1, 1)
        copied2 = keep.tile([P, POOL_SHARE2], F32, name="copied2", align_bytes=64)
        nc.scalar.copy(copied2[:], sums[2, 0][:, 0:POOL_SHARE2])
        finish_low(2, 4)
        finish_low(3, 5)
        high = {
            2: keep.tile([P, ROW_TILES, SLICE], F32, name="res2", tag="scaled", align_bytes=64),
        }
        gather_ts(2, 3, reuse="picked2_1")
        second_late = keep.tile([P, LATE], U32, name="second_late", tag="copied", align_bytes=64)
        nc.vector.tensor_copy(second_late[:], table[SECOND][:].bitcast(U32).indirect(offsets[:, (S - LATE) // 16 : S // 16]))
        gather_words(LAST, 3, 4, reuse="picked_ts1")
        sum_direct(2, 2, 6)
        sum_direct(2, 3, 7)
        y_second = keep.tile([P, POOL_SHARE2], F32, name="y_second", tag="table%d" % LAST, align_bytes=64)
        nc.gpsimd.tensor_tensor(y_second[:], copied2[:], picked_ts[2][:, 0:POOL_SHARE2], MULT)
        finish_high(2, 1)
        finish_high(2, 2)
        nc.scalar.activation(high[2][:, 0, 0:POOL_SHARE2], y_second[:], GELU, bias=bias[:, 0:1])
        store(high[2][:, 0, :], 0, 2 * SLICE, 3 * SLICE)
        finish_high(2, 3)
        high[3] = keep.tile([P, ROW_TILES, SLICE], F32, name="res3", align_bytes=64)
        gather_ts(3, 4, reuse="picked2_2", pieces=2)
        for m in range(ROW_TILES):
            sum_direct(3, m, 2 + m)
            finish_high(3, m, 2)
